import numpy as np
import ml_dtypes


def mxq(x, axis, fmt="e4m3"):
    dtype, down = {"e4m3": (ml_dtypes.float8_e4m3fn, 7), "e5m2": (ml_dtypes.float8_e5m2, 14)}[fmt]
    v = np.moveaxis(np.asarray(x, np.float32).astype(ml_dtypes.bfloat16).astype(np.float64), axis, -1)
    blocks = v.reshape(v.shape[:-1] + (-1, 32))
    amax = np.abs(blocks).max(-1, keepdims=True)
    byte = np.maximum(np.where(amax > 0, np.frexp(amax)[1] - 1 + 127, 0) - down, 1)
    scale = np.exp2(byte - 127.0)
    codes = (blocks / scale).astype(np.float32).astype(dtype).astype(np.float64)
    return np.moveaxis((codes * scale).reshape(v.shape), -1, axis)


WIDE = False


def mx_kscale(k):
    if not WIDE:
        return np.ones(k)
    levels = np.array([10, -10, 5, -5, 0])
    if k % 512:
        return np.exp2(np.random.permutation(np.resize(levels, k // 32))).repeat(32)
    a = np.empty((k // 512, 16))
    for p in range(k // 512):
        a[p, :8] = np.random.permutation(np.resize(levels, 8))
        for g in range(8):
            far = levels[np.abs(levels - a[p, g]) >= 10]
            a[p, g + 8] = far[np.random.randint(len(far))]
    return np.exp2(a.ravel()).repeat(32)


BF16 = ml_dtypes.bfloat16


def bf(x):
    return np.asarray(x, np.float32).astype(BF16)


def f64(x):
    return np.asarray(x).astype(np.float64)


E2M1 = np.array([0.0, 0.5, 1.0, 1.5, 2.0, 3.0, 4.0, 6.0, -0.0, -0.5, -1.0, -1.5, -2.0, -3.0, -4.0, -6.0])


def pack_weight(w, fmt):
    k, n = w.shape
    w = f64(bf(w)).reshape(k // 32, 32, n)
    amax = np.abs(w).max(1)
    if fmt == "e4m3":
        byte = np.frexp(amax)[1] - 1 + 127 - 7
    else:
        mant, ex = np.frexp(amax / 6.0)
        byte = np.where(mant > 0.5, ex, ex - 1) + 127
    byte = np.clip(np.where(amax > 0, byte, 1), 1, 254)
    scaled = (w * np.exp2(127.0 - byte)[:, None, :]).reshape(k, n).astype(np.float32)
    by_word = np.ascontiguousarray(scaled.reshape(k // 512, 128, 4, n).transpose(0, 1, 3, 2))
    if fmt == "e4m3":
        words = by_word.astype(ml_dtypes.float8_e4m3fn).view(np.uint8)
    else:
        c = by_word.astype(ml_dtypes.float4_e2m1fn).view(np.uint8) & 0xF
        words = c[..., 0::2] | (c[..., 1::2] << 4)
    return np.ascontiguousarray(words), np.ascontiguousarray(byte.astype(np.uint8).reshape(k // 512, 16, n))


def unpack_weight(words, scales, fmt):
    g, p, n, _ = words.shape
    if fmt == "e4m3":
        vals = np.ascontiguousarray(words).view(ml_dtypes.float8_e4m3fn).astype(np.float64)
    else:
        nib = np.empty((g, p, n, 4), np.uint8)
        nib[..., 0::2] = words & 0xF
        nib[..., 1::2] = words >> 4
        vals = E2M1[nib]
    vals = vals * np.repeat(np.exp2(scales.astype(np.float64) - 127.0), 8, axis=1)[..., None]
    return vals.transpose(0, 1, 3, 2).reshape(g * 512, n)
def pack4(w):
    words, scales = pack_weight(w, "e2m1")
    return words.reshape(words.shape[0], 128, -1), scales


def unpack4(words, scales):
    return unpack_weight(words.reshape(words.shape[0], 128, -1, 2), scales, "e2m1")


E4M3FN = np.array([(-1.0 if i & 128 else 1.0) * ((1.0 + (i & 7) / 8.0) * 2.0 ** (((i >> 3) & 15) - 7) if i & 120 else (i & 7) * 2.0 ** -9) for i in range(256)])


def e4m3fn_bytes(y):
    return np.clip(np.asarray(y, np.float64), -448.0, 448.0).astype(np.float32).astype(ml_dtypes.float8_e4m3fn).view(np.uint8)


def e4m3fn_values(b):
    return E4M3FN[b]

def planes(Y):
    n, m = Y.shape
    b = f64(bf(Y)).reshape(n // 32, 32, m)
    amax = np.abs(b).max(1)
    byte = np.clip(np.where(amax > 0, np.frexp(amax)[1] - 1 + 127 - 7, 1), 1, 254)
    codes = (b * np.exp2(127.0 - byte)[:, None, :]).reshape(n, m).astype(np.float32).astype(ml_dtypes.float8_e4m3fn).view(np.uint8)
    words = codes.reshape(n // 512, 128, 4, m).transpose(0, 1, 3, 2)
    return np.ascontiguousarray(words), np.ascontiguousarray(byte.astype(np.uint8).reshape(n // 512, 16, m))


G, T, L, F, Q = 4, 384, 1024, 512, 128

def setup_inputs():
    s, t = mx_kscale(L), mx_kscale(L)
    X = np.random.randn(G, T, L) * np.exp(0.4 * np.random.randn(G, T, 1)) * s
    X_scale = (np.abs(X).reshape(G, T, L // Q, Q).max(axis=3) / 448).astype(np.float32)
    X_bytes = e4m3fn_bytes(X / np.repeat(f64(X_scale), Q, axis=2))
    A = np.random.randn(G, L, L) / np.sqrt(L) / s[:, None]
    A_words, A_scales = pack4(A.reshape(G * L, L))
    rate = 1 + 0.002 * np.random.randn(G, 1, 1)
    angle = 2 * np.pi * rate * np.arange(L)[:, None] * (np.arange(F) + 0.5) / L
    C = np.cos(angle) * np.sqrt(2 / L) / t[:, None]
    S = np.sin(angle) * np.sqrt(2 / L) / t[:, None]
    C_words, C_scales = pack4(C.reshape(G * L, F))
    S_words, S_scales = pack4(S.reshape(G * L, F))
    hamming = 0.54 - 0.46 * np.cos(2 * np.pi * (np.arange(L) + 0.5) / L)
    window = hamming * (1 + 0.1 * np.random.randn(G, L)) * t
    gain = np.exp(0.8 * np.random.randn(G, F))
    return {"X_bytes": X_bytes, "X_scale": X_scale, "A_words": A_words, "A_scales": A_scales,
            "C_words": C_words, "C_scales": C_scales, "S_words": S_words, "S_scales": S_scales,
            "window": bf(window), "gain": bf(gain)}

def reference(X_bytes, X_scale, A_words, A_scales, C_words, C_scales, S_words, S_scales, window, gain):
    X = e4m3fn_values(X_bytes) * np.repeat(f64(X_scale), Q, axis=2)
    A = unpack4(A_words, A_scales).reshape(G, L, L)
    C = unpack4(C_words, C_scales).reshape(G, L, F)
    S = unpack4(S_words, S_scales).reshape(G, L, F)
    h = (mxq(X, 2, "e4m3") @ A) * f64(window)[:, None, :]
    hq = mxq(h, 2, "e4m3")
    re = hq @ C
    im = hq @ S
    y = np.sqrt(re * re + im * im) * f64(gain)[:, None, :]
    words, scales = planes(y.reshape(G * T, F).T)
    return y, words, scales

@@ -1,0 +1,312 @@
+from contextlib import ExitStack
+
+import concourse.mybir as mybir
+from concourse.masks import make_identity
+
+G, T, L, F, Q = 4, 384, 1024, 512, 128
+FLOPS = 2 * G * T * L * (L + 2 * F)
+
+F32 = mybir.dt.float32
+BF16 = mybir.dt.bfloat16
+I32 = mybir.dt.int32
+U32 = mybir.dt.uint32
+U8 = mybir.dt.uint8
+FP8 = mybir.dt.float8_e4m3fn
+FP8X4 = mybir.dt.float8_e4m3fn_x4
+FP4X4 = mybir.dt.float4_e2m1fn_x4
+ACT = mybir.ActivationFunctionType
+ALU = mybir.AluOpType
+
+P = 128
+K_PASS = 512
+PASSES = L // K_PASS
+TILES_PER_MIC = T // P
+TILES = G * TILES_PER_MIC
+BLOCKS_PER_PASS = K_PASS // Q
+ROUND_ON_VECTOR_FROM = 7
+STORE_AFTER = {2: 0, 5: 3, 8: 6, 10: 9, 11: 11}
+
+
+def tile_mic_spectrogram_magnitudes_b12_kernel(
+    tc, X_bytes, X_scale, A_words, A_scales, C_words, C_scales, S_words, S_scales, window, gain, out_0, out_1, out_2
+):
+    nc = tc.nc
+    with ExitStack() as ctx:
+        sb = ctx.enter_context(tc.tile_pool(name="sb", bufs=1))
+        ps = ctx.enter_context(tc.psum_pool(name="ps", bufs=1))
+        ctx.enter_context(tc.manual_schedule())
+
+        def ring(name, depth, shape, dtype):
+            return [sb.tile(shape, dtype, name="%s%d" % (name, j), align_bytes=64) for j in range(depth)]
+
+        ident = sb.tile([P, P], F32, name="ident")
+        make_identity(nc, ident[:])
+
+        warm = sb.tile([P, 8], F32, name="warm")
+        warm_out = sb.tile([P, 8], F32, name="warm_out")
+        nc.vector.memset(warm[:], 1.0)
+        nc.scalar.activation(out=warm_out[:], in_=warm[:], func=ACT.Sqrt)
+
+        weights = {"A": (A_words, A_scales, L), "C": (C_words, C_scales, F), "S": (S_words, S_scales, F)}
+        mic_runs = [(0, 1), (1, G)]
+        planes = {}
+        for first, last in mic_runs:
+            for name, (words, scales, width) in weights.items():
+                plane = sb.tile([P, (last - first) * PASSES * width], U8, name="%s_plane%d" % (name, first), align_bytes=64)
+                nc.vector.memset(plane[:].bitcast(I32), 0)
+                planes[name, first] = plane
+
+        def load_scales(name, first, last):
+            words, scales, width = weights[name]
+            plane = planes[name, first]
+            for quad in range(4):
+                nc.sync.dma_start(
+                    out=plane[32 * quad : 32 * quad + 4, :].bitcast(I32).rearrange("r (g n) -> r g n", n=width // 4),
+                    in_=scales[PASSES * first : PASSES * last, 4 * quad : 4 * quad + 4, :]
+                    .bitcast(I32)
+                    .rearrange("g r n -> r g n"),
+                )
+
+        codes4 = {}
+
+        def load_words(name, mic):
+            words, scales, width = weights[name]
+            tile4 = sb.tile([P, PASSES * 2 * width], U8, name="%s_words%d" % (name, mic), align_bytes=64)
+            nc.sync.dma_start(
+                out=tile4[:].bitcast(I32).rearrange("p (g n) -> p g n", g=PASSES),
+                in_=words[PASSES * mic : PASSES * (mic + 1)].bitcast(I32).rearrange("g p n -> p g n"),
+            )
+            codes4[name, mic] = tile4
+
+        def weight_operand(name, mic, g, col0):
+            width = weights[name][2]
+            first = min(mic, 1)
+            byte0 = 2 * (g * width + col0)
+            scale0 = (PASSES * (mic - first) + g) * width + col0
+            return (
+                codes4[name, mic][:, byte0 : byte0 + 2 * K_PASS].bitcast(FP4X4),
+                planes[name, first][:, scale0 : scale0 + K_PASS],
+            )
+
+        frames = {}
+
+        def load_frames(first, last):
+            mic, t0 = divmod(first, TILES_PER_MIC)
+            count = last - first
+            raw = sb.tile([P, count, L], U8, name="frame_bytes%d" % first, align_bytes=64)
+            nc.sync.dma_start(
+                out=raw[:],
+                in_=X_bytes[mic, P * t0 : P * (t0 + count), :].rearrange("(t p) k -> p t k", p=P),
+            )
+            for j in range(count):
+                frames[first + j] = (raw, j)
+
+        spread = {}
+
+        def load_spread(name, rows, first, last):
+            width = rows.shape[1]
+            wide = sb.tile([P, (last - first) * width], BF16, name="%s_spread%d" % (name, first), align_bytes=64)
+            nc.sync.dma_start(out=wide[:], in_=rows[first:last].rearrange("g n -> (g n)").partition_broadcast(P))
+            for mic in range(first, last):
+                spread[name, mic] = (wide, (mic - first) * width)
+
+        scale_rows = X_scale.rearrange("g (t p) b -> p (g t) b", p=P)
+        x_scale_first = sb.tile([P, 1, L // Q], F32, name="x_scale_first")
+        x_scale_rest = sb.tile([P, TILES - 1, L // Q], F32, name="x_scale_rest")
+        load_frames(0, 1)
+        nc.sync.dma_start(out=x_scale_first[:], in_=scale_rows[:, 0:1, :])
+        load_frames(1, TILES_PER_MIC)
+        nc.sync.dma_start(out=x_scale_rest[:], in_=scale_rows[:, 1:TILES, :])
+        load_scales("A", 0, 1)
+        load_words("A", 0)
+        load_spread("window", window, 0, 1)
+        load_frames(TILES_PER_MIC, 2 * TILES_PER_MIC)
+        load_scales("C", 0, 1)
+        load_scales("S", 0, 1)
+        load_words("C", 0)
+        load_words("S", 0)
+        load_spread("gain", gain, 0, G)
+        load_scales("A", 1, G)
+        load_words("A", 1)
+        load_spread("window", window, 1, G)
+        load_scales("C", 1, G)
+        load_scales("S", 1, G)
+        load_words("C", 1)
+        load_words("S", 1)
+        for mic in range(2, G):
+            load_frames(mic * TILES_PER_MIC, (mic + 1) * TILES_PER_MIC)
+            for name in weights:
+                load_words(name, mic)
+
+        x_wide = [ring("x_wide%d_" % g, 3, [P, K_PASS], BF16) for g in range(PASSES)]
+        x_grouped = ring("x_grouped", 2, [P, L], BF16)
+        x_codes = ring("x_codes", 2, [P, PASSES * P], U32)
+        x_planes = ring("x_planes", 2, [P, PASSES * P], U8)
+        h_wide = [ring("h_wide%d_" % g, 2, [P, K_PASS], BF16) for g in range(PASSES)]
+        h_grouped = ring("h_grouped", 2, [P, L], BF16)
+        h_codes = ring("h_codes", 2, [P, PASSES * P], U32)
+        h_planes = ring("h_planes", 2, [P, PASSES * P], U8)
+        re_sq = ring("re_sq", 2, [P, F], F32)
+        im_sq = ring("im_sq", 2, [P, F], F32)
+        power = ring("power", 2, [P, F], F32)
+        magnitude = ring("magnitude", 2, [P, F], F32)
+        y_full = ring("y_full", 4, [P, F], F32)
+        y_half = ring("y_half", 2, [P, F], BF16)
+        y_grouped = ring("y_grouped", 2, [P, F], BF16)
+        y_codes = sb.tile([P, TILES * P], U32, name="y_codes", align_bytes=64)
+        y_plane = sb.tile([P, TILES * P], U8, name="y_plane", align_bytes=64)
+
+        x_turned = ps.tile([P, 2 * PASSES * P], F32, name="x_turned")
+        h_turned = [ps.tile([P, 2 * PASSES * P], F32, name="h_turned%d" % j) for j in range(2)]
+        y_turned = ps.tile([P, 2 * P], F32, name="y_turned")
+        h_sum = [ps.tile([P, K_PASS], F32, name="h_sum%d" % g) for g in range(PASSES)]
+        re_sum = ps.tile([P, F], F32, name="re_sum")
+        im_sum = ps.tile([P, F], F32, name="im_sum")
+
+        def slot(tiles, i):
+            return tiles[i % len(tiles)]
+
+        def by_pairs(ap):
+            return ap.rearrange("p (q u e) -> p u q e", u=2, e=2)
+
+        def sorted_pairs(ap):
+            return ap.rearrange("p (u q e) -> p u q e", u=2, e=2)
+
+        def widen(i, g):
+            raw, j = frames[i]
+            row_scales = x_scale_first[:, 0, :] if i == 0 else x_scale_rest[:, i - 1, :]
+            target = slot(x_wide[g], i)[:].rearrange("p (u q e) -> p q u e", u=2, e=2)
+            for b in range(BLOCKS_PER_PASS):
+                block = BLOCKS_PER_PASS * g + b
+                nc.vector.tensor_scalar(
+                    out=target[:, 32 * b : 32 * (b + 1), :, :],
+                    in0=raw[:, j, Q * block : Q * (block + 1)].bitcast(FP8).rearrange("p (q u e) -> p q u e", u=2, e=2),
+                    scalar1=row_scales[:, block : block + 1],
+                    scalar2=None,
+                    op0=ALU.mult,
+                )
+
+        def turn(bank, halves):
+            for g, half in enumerate(halves):
+                words = half[:].bitcast(F32)
+                for u in range(2):
+                    col = (2 * g + u) * P
+                    nc.tensor.transpose(bank[:, col : col + P], words[:, u * P : (u + 1) * P], ident[:])
+
+        def group(copy, grouped, bank):
+            copy(
+                out=grouped[:].bitcast(F32).rearrange("p (g r u) -> p g r u", r=P, u=2),
+                in_=bank[:].rearrange("p (g u r) -> p g r u", r=P, u=2),
+            )
+
+        def quantize(codes, plane, grouped):
+            nc.vector.quantize_mx(out=codes.bitcast(FP8X4), scales=plane, in_=grouped[:])
+
+        def multiply(acc, codes, plane, name, i, col0):
+            for g in range(PASSES):
+                rhs, rhs_scale = weight_operand(name, i // TILES_PER_MIC, g, col0)
+                nc.tensor.matmul_mx(
+                    out=acc[:],
+                    lhsT=codes[:, g * P : (g + 1) * P].bitcast(FP8X4),
+                    lhsT_scale=plane[:, g * P : (g + 1) * P],
+                    rhs=rhs,
+                    rhs_scale=rhs_scale,
+                    start=(g == 0),
+                    stop=(g == PASSES - 1),
+                )
+
+        def apply_window(i, g):
+            wide, col0 = spread["window", i // TILES_PER_MIC]
+            col = col0 + g * K_PASS
+            nc.vector.tensor_tensor(
+                out=sorted_pairs(slot(h_wide[g], i)[:]),
+                in0=by_pairs(h_sum[g][:]),
+                in1=by_pairs(wide[:, col : col + K_PASS]),
+                op=ALU.mult,
+            )
+
+        def apply_gain(i):
+            wide, col0 = spread["gain", i // TILES_PER_MIC]
+            nc.vector.tensor_tensor(
+                out=slot(y_full, i)[:], in0=slot(magnitude, i)[:], in1=wide[:, col0 : col0 + F], op=ALU.mult
+            )
+            mic, t = divmod(i, TILES_PER_MIC)
+            nc.sync.dma_start(out=out_0[mic, P * t : P * (t + 1), :], in_=slot(y_full, i)[:])
+
+        words_out = out_1[0].rearrange("p m t -> p (m t)").bitcast(I32)
+
+        def store_codes(first, last):
+            nc.sync.dma_start(out=words_out[:, P * first : P * last], in_=y_codes[:, P * first : P * last].bitcast(I32))
+
+        def live(i):
+            return 0 <= i < TILES
+
+        def x_halves(i):
+            return [slot(x_wide[g], i) for g in range(PASSES)]
+
+        def h_halves(i):
+            return [slot(h_wide[g], i) for g in range(PASSES)]
+
+        def round_y(i):
+            copy = nc.vector.tensor_copy if i >= ROUND_ON_VECTOR_FROM else nc.scalar.copy
+            copy(out=sorted_pairs(slot(y_half, i)[:]), in_=by_pairs(slot(y_full, i)[:]))
+
+        def quantize_y(i):
+            quantize(y_codes[:, P * i : P * (i + 1)], y_plane[:, P * i : P * (i + 1)], slot(y_grouped, i))
+            if i in STORE_AFTER:
+                store_codes(STORE_AFTER[i], i + 1)
+
+        for s in range(-2, TILES + 5):
+            if live(s - 1):
+                turn(slot(h_turned, s - 1), h_halves(s - 1))
+            if live(s - 2):
+                nc.scalar.activation(out=slot(im_sq, s - 2)[:], in_=im_sum[:], func=ACT.Square)
+            if live(s):
+                quantize(slot(x_codes, s)[:], slot(x_planes, s)[:], slot(x_grouped, s))
+            if live(s + 1):
+                turn(x_turned, x_halves(s + 1))
+            if live(s - 5):
+                quantize_y(s - 5)
+            if live(s - 4):
+                turn(y_turned, [slot(y_half, s - 4)])
+            if live(s + 2):
+                widen(s + 2, 0)
+                widen(s + 2, 1)
+            if live(s - 1):
+                group(nc.scalar.copy, slot(h_grouped, s - 1), slot(h_turned, s - 1))
+            if live(s - 2):
+                nc.vector.tensor_tensor(
+                    out=slot(power, s - 2)[:], in0=slot(re_sq, s - 2)[:], in1=slot(im_sq, s - 2)[:], op=ALU.add
+                )
+            if live(s):
+                for g in range(PASSES):
+                    multiply(h_sum[g], slot(x_codes, s), slot(x_planes, s), "A", s, g * K_PASS)
+            if live(s + 1):
+                group(nc.scalar.copy, slot(x_grouped, s + 1), x_turned)
+            if live(s - 1):
+                quantize(slot(h_codes, s - 1)[:], slot(h_planes, s - 1)[:], slot(h_grouped, s - 1))
+            if live(s - 4):
+                copy = nc.vector.tensor_copy if s - 4 == TILES - 1 else nc.scalar.copy
+                group(copy, slot(y_grouped, s - 4), y_turned)
+            if live(s):
+                apply_window(s, 0)
+            if live(s - 1):
+                multiply(re_sum, slot(h_codes, s - 1), slot(h_planes, s - 1), "C", s - 1, 0)
+                multiply(im_sum, slot(h_codes, s - 1), slot(h_planes, s - 1), "S", s - 1, 0)
+            if live(s - 2):
+                nc.scalar.activation(out=slot(magnitude, s - 2)[:], in_=slot(power, s - 2)[:], func=ACT.Sqrt)
+            if live(s):
+                apply_window(s, 1)
+            if live(s - 3):
+                round_y(s - 3)
+            if live(s - 2):
+                apply_gain(s - 2)
+            if live(s - 1):
+                nc.scalar.activation(out=slot(re_sq, s - 1)[:], in_=re_sum[:], func=ACT.Square)
+
+        for quad in range(4):
+            queue = nc.scalar if quad % 2 == 0 else nc.sync
+            queue.dma_start(
+                out=out_2[0, 4 * quad : 4 * quad + 4, :].bitcast(I32),
+                in_=y_plane[32 * quad : 32 * quad + 4, :].bitcast(I32),
+            )

@@ -23,7 +23,7 @@ PASSES = L // K_PASS
 TILES_PER_MIC = T // P
 TILES = G * TILES_PER_MIC
 BLOCKS_PER_PASS = K_PASS // Q
-ROUND_ON_VECTOR_FROM = 7
+ROUND_ON_VECTOR_FROM = 6
 STORE_AFTER = {2: 0, 5: 3, 8: 6, 10: 9, 11: 11}
 
 
@@ -138,7 +138,7 @@ def tile_mic_spectrogram_magnitudes_b12_kernel(
             for name in weights:
                 load_words(name, mic)
 
-        x_wide = [ring("x_wide%d_" % g, 3, [P, K_PASS], BF16) for g in range(PASSES)]
+        x_wide = [ring("x_wide%d_" % g, 4, [P, K_PASS], BF16) for g in range(PASSES)]
         x_grouped = ring("x_grouped", 2, [P, L], BF16)
         x_codes = ring("x_codes", 2, [P, PASSES * P], U32)
         x_planes = ring("x_planes", 2, [P, PASSES * P], U8)
@@ -175,16 +175,22 @@ def tile_mic_spectrogram_magnitudes_b12_kernel(
         def widen(i, g):
             raw, j = frames[i]
             row_scales = x_scale_first[:, 0, :] if i == 0 else x_scale_rest[:, i - 1, :]
-            target = slot(x_wide[g], i)[:].rearrange("p (u q e) -> p q u e", u=2, e=2)
             for b in range(BLOCKS_PER_PASS):
                 block = BLOCKS_PER_PASS * g + b
-                nc.vector.tensor_scalar(
-                    out=target[:, 32 * b : 32 * (b + 1), :, :],
-                    in0=raw[:, j, Q * block : Q * (block + 1)].bitcast(FP8).rearrange("p (q u e) -> p q u e", u=2, e=2),
-                    scalar1=row_scales[:, block : block + 1],
-                    scalar2=None,
-                    op0=ALU.mult,
-                )
+                target = slot(x_wide[g], i)[:, Q * b : Q * (b + 1)]
+                codes = raw[:, j, Q * block : Q * (block + 1)].bitcast(FP8)
+                scale = row_scales[:, block : block + 1]
+                if (i, g) == (0, 1):
+                    nc.scalar.activation(out=target, in_=codes, func=ACT.Copy, scale=scale)
+                else:
+                    nc.vector.tensor_scalar(out=target, in0=codes, scalar1=scale, scalar2=None, op0=ALU.mult)
+
+        def turn_frames(bank, halves):
+            for g, half in enumerate(halves):
+                words = half[:].bitcast(F32)
+                for u in range(2):
+                    col = (2 * g + u) * P
+                    nc.tensor.transpose(bank[:, col : col + P], words[:, u : 2 * P : 2], ident[:])
 
         def turn(bank, halves):
             for g, half in enumerate(halves):
@@ -195,15 +201,15 @@ def tile_mic_spectrogram_magnitudes_b12_kernel(
 
         def group(copy, grouped, bank):
             copy(
-                out=grouped[:].bitcast(F32).rearrange("p (g r u) -> p g r u", r=P, u=2),
-                in_=bank[:].rearrange("p (g u r) -> p g r u", r=P, u=2),
+                out=grouped.bitcast(F32).rearrange("p (g r u) -> p g r u", r=P, u=2),
+                in_=bank.rearrange("p (g u r) -> p g r u", r=P, u=2),
             )
 
         def quantize(codes, plane, grouped):
-            nc.vector.quantize_mx(out=codes.bitcast(FP8X4), scales=plane, in_=grouped[:])
+            nc.vector.quantize_mx(out=codes.bitcast(FP8X4), scales=plane, in_=grouped)
 
-        def multiply(acc, codes, plane, name, i, col0):
-            for g in range(PASSES):
+        def multiply(acc, codes, plane, name, i, col0, passes=range(PASSES)):
+            for g in passes:
                 rhs, rhs_scale = weight_operand(name, i // TILES_PER_MIC, g, col0)
                 nc.tensor.matmul_mx(
                     out=acc[:],
@@ -225,13 +231,16 @@ def tile_mic_spectrogram_magnitudes_b12_kernel(
                 op=ALU.mult,
             )
 
-        def apply_gain(i):
+        def apply_gain(i, cols=slice(0, F)):
             wide, col0 = spread["gain", i // TILES_PER_MIC]
             nc.vector.tensor_tensor(
-                out=slot(y_full, i)[:], in0=slot(magnitude, i)[:], in1=wide[:, col0 : col0 + F], op=ALU.mult
+                out=slot(y_full, i)[:, cols],
+                in0=slot(magnitude, i)[:, cols],
+                in1=wide[:, col0 + cols.start : col0 + cols.stop],
+                op=ALU.mult,
             )
             mic, t = divmod(i, TILES_PER_MIC)
-            nc.sync.dma_start(out=out_0[mic, P * t : P * (t + 1), :], in_=slot(y_full, i)[:])
+            nc.sync.dma_start(out=out_0[mic, P * t : P * (t + 1), cols], in_=slot(y_full, i)[:, cols])
 
         words_out = out_1[0].rearrange("p m t -> p (m t)").bitcast(I32)
 
@@ -247,54 +256,69 @@ def tile_mic_spectrogram_magnitudes_b12_kernel(
         def h_halves(i):
             return [slot(h_wide[g], i) for g in range(PASSES)]
 
-        def round_y(i):
+        def round_y(i, cols=slice(0, F)):
             copy = nc.vector.tensor_copy if i >= ROUND_ON_VECTOR_FROM else nc.scalar.copy
-            copy(out=sorted_pairs(slot(y_half, i)[:]), in_=by_pairs(slot(y_full, i)[:]))
+            quads = slice(cols.start // 4, cols.stop // 4)
+            copy(out=sorted_pairs(slot(y_half, i)[:])[:, :, quads, :], in_=by_pairs(slot(y_full, i)[:, cols]))
 
         def quantize_y(i):
-            quantize(y_codes[:, P * i : P * (i + 1)], y_plane[:, P * i : P * (i + 1)], slot(y_grouped, i))
+            quantize(y_codes[:, P * i : P * (i + 1)], y_plane[:, P * i : P * (i + 1)], slot(y_grouped, i)[:])
             if i in STORE_AFTER:
                 store_codes(STORE_AFTER[i], i + 1)
 
-        for s in range(-2, TILES + 5):
+        def square(squares, sums, i, cols=slice(0, F)):
+            nc.scalar.activation(out=slot(squares, i)[:, cols], in_=sums[:, cols], func=ACT.Square)
+
+        def add_squares(i, cols=slice(0, F)):
+            nc.vector.tensor_tensor(
+                out=slot(power, i)[:, cols], in0=slot(re_sq, i)[:, cols], in1=slot(im_sq, i)[:, cols], op=ALU.add
+            )
+
+        def root(i, cols=slice(0, F)):
+            nc.scalar.activation(out=slot(magnitude, i)[:, cols], in_=slot(power, i)[:, cols], func=ACT.Sqrt)
+
+        def turn_y(i):
+            turn(y_turned, [slot(y_half, i)])
+
+        def group_y(copy, i):
+            group(copy, slot(y_grouped, i)[:], y_turned[:])
+
+        for s in range(-3, TILES):
             if live(s - 1):
                 turn(slot(h_turned, s - 1), h_halves(s - 1))
             if live(s - 2):
-                nc.scalar.activation(out=slot(im_sq, s - 2)[:], in_=im_sum[:], func=ACT.Square)
+                square(im_sq, im_sum, s - 2)
             if live(s):
-                quantize(slot(x_codes, s)[:], slot(x_planes, s)[:], slot(x_grouped, s))
+                quantize(slot(x_codes, s)[:], slot(x_planes, s)[:], slot(x_grouped, s)[:])
             if live(s + 1):
-                turn(x_turned, x_halves(s + 1))
+                turn_frames(x_turned, x_halves(s + 1))
             if live(s - 5):
                 quantize_y(s - 5)
             if live(s - 4):
-                turn(y_turned, [slot(y_half, s - 4)])
-            if live(s + 2):
-                widen(s + 2, 0)
-                widen(s + 2, 1)
+                turn_y(s - 4)
+            if live(s + 3):
+                widen(s + 3, 0)
+                widen(s + 3, 1)
             if live(s - 1):
-                group(nc.scalar.copy, slot(h_grouped, s - 1), slot(h_turned, s - 1))
+                group(nc.scalar.copy, slot(h_grouped, s - 1)[:], slot(h_turned, s - 1)[:])
             if live(s - 2):
-                nc.vector.tensor_tensor(
-                    out=slot(power, s - 2)[:], in0=slot(re_sq, s - 2)[:], in1=slot(im_sq, s - 2)[:], op=ALU.add
-                )
+                add_squares(s - 2)
             if live(s):
                 for g in range(PASSES):
                     multiply(h_sum[g], slot(x_codes, s), slot(x_planes, s), "A", s, g * K_PASS)
             if live(s + 1):
-                group(nc.scalar.copy, slot(x_grouped, s + 1), x_turned)
+                group(nc.scalar.copy, slot(x_grouped, s + 1)[:], x_turned[:])
             if live(s - 1):
-                quantize(slot(h_codes, s - 1)[:], slot(h_planes, s - 1)[:], slot(h_grouped, s - 1))
+                quantize(slot(h_codes, s - 1)[:], slot(h_planes, s - 1)[:], slot(h_grouped, s - 1)[:])
             if live(s - 4):
-                copy = nc.vector.tensor_copy if s - 4 == TILES - 1 else nc.scalar.copy
-                group(copy, slot(y_grouped, s - 4), y_turned)
+                group_y(nc.scalar.copy, s - 4)
             if live(s):
                 apply_window(s, 0)
             if live(s - 1):
                 multiply(re_sum, slot(h_codes, s - 1), slot(h_planes, s - 1), "C", s - 1, 0)
                 multiply(im_sum, slot(h_codes, s - 1), slot(h_planes, s - 1), "S", s - 1, 0)
             if live(s - 2):
-                nc.scalar.activation(out=slot(magnitude, s - 2)[:], in_=slot(power, s - 2)[:], func=ACT.Sqrt)
+                root(s - 2)
             if live(s):
                 apply_window(s, 1)
             if live(s - 3):
@@ -302,7 +326,61 @@ def tile_mic_spectrogram_magnitudes_b12_kernel(
             if live(s - 2):
                 apply_gain(s - 2)
             if live(s - 1):
-                nc.scalar.activation(out=slot(re_sq, s - 1)[:], in_=re_sum[:], func=ACT.Square)
+                square(re_sq, re_sum, s - 1)
+
+        last = TILES - 1
+        banks = [slot(h_turned, last), x_turned]
+        low, high = slice(0, F // 2), slice(F // 2, F)
+
+        def group_last(g):
+            group(nc.scalar.copy, slot(h_grouped, last)[:, g * K_PASS : (g + 1) * K_PASS], banks[g][:, 0 : 2 * P])
+
+        def quantize_last(g):
+            quantize(
+                slot(h_codes, last)[:, g * P : (g + 1) * P],
+                slot(h_planes, last)[:, g * P : (g + 1) * P],
+                slot(h_grouped, last)[:, g * K_PASS : (g + 1) * K_PASS],
+            )
+
+        for g in range(PASSES):
+            turn(banks[g], [slot(h_wide[g], last)])
+        square(im_sq, im_sum, last - 1)
+        quantize_y(last - 4)
+        turn_y(last - 3)
+        group_last(0)
+        add_squares(last - 1)
+        group_last(1)
+        quantize_last(0)
+        round_y(last - 2)
+        quantize_last(1)
+        for g in range(PASSES):
+            multiply(re_sum, slot(h_codes, last), slot(h_planes, last), "C", last, 0, [g])
+            multiply(im_sum, slot(h_codes, last), slot(h_planes, last), "S", last, 0, [g])
+        root(last - 1)
+        group_y(nc.scalar.copy, last - 3)
+        turn_y(last - 2)
+        apply_gain(last - 1)
+        for cols in (low, high):
+            square(re_sq, re_sum, last, cols)
+            square(im_sq, im_sum, last, cols)
+        quantize_y(last - 3)
+        group_y(nc.vector.tensor_copy, last - 2)
+        add_squares(last, low)
+        round_y(last - 1)
+        add_squares(last, high)
+        root(last, low)
+        root(last, high)
+        turn_y(last - 1)
+        quantize_y(last - 2)
+        apply_gain(last, low)
+        group_y(nc.scalar.copy, last - 1)
+        apply_gain(last, high)
+        round_y(last, low)
+        round_y(last, high)
+        turn_y(last)
+        quantize_y(last - 1)
+        group_y(nc.vector.tensor_copy, last)
+        quantize_y(last)
 
         for quad in range(4):
             queue = nc.scalar if quad % 2 == 0 else nc.sync

@@ -23,7 +23,7 @@ PASSES = L // K_PASS
 TILES_PER_MIC = T // P
 TILES = G * TILES_PER_MIC
 BLOCKS_PER_PASS = K_PASS // Q
-ROUND_ON_VECTOR_FROM = 6
+ROUND_ON_VECTOR_FROM = 7
 STORE_AFTER = {2: 0, 5: 3, 8: 6, 10: 9, 11: 11}
 
 
@@ -48,17 +48,18 @@ def tile_mic_spectrogram_magnitudes_b12_kernel(
         nc.scalar.activation(out=warm_out[:], in_=warm[:], func=ACT.Sqrt)
 
         weights = {"A": (A_words, A_scales, L), "C": (C_words, C_scales, F), "S": (S_words, S_scales, F)}
-        mic_runs = [(0, 1), (1, G)]
         planes = {}
-        for first, last in mic_runs:
-            for name, (words, scales, width) in weights.items():
-                plane = sb.tile([P, (last - first) * PASSES * width], U8, name="%s_plane%d" % (name, first), align_bytes=64)
-                nc.vector.memset(plane[:].bitcast(I32), 0)
-                planes[name, first] = plane
+
+        def clear_plane(name, first, last):
+            width = weights[name][2]
+            plane = sb.tile([P, (last - first) * PASSES * width], U8, name="%s_plane%d" % (name, first), align_bytes=64)
+            nc.vector.memset(plane[:].bitcast(I32), 0)
+            for mic in range(first, last):
+                planes[name, mic] = (plane, first)
 
         def load_scales(name, first, last):
-            words, scales, width = weights[name]
-            plane = planes[name, first]
+            scales, width = weights[name][1:]
+            plane = planes[name, first][0]
             for quad in range(4):
                 nc.sync.dma_start(
                     out=plane[32 * quad : 32 * quad + 4, :].bitcast(I32).rearrange("r (g n) -> r g n", n=width // 4),
@@ -80,12 +81,12 @@ def tile_mic_spectrogram_magnitudes_b12_kernel(
 
         def weight_operand(name, mic, g, col0):
             width = weights[name][2]
-            first = min(mic, 1)
+            plane, first = planes[name, mic]
             byte0 = 2 * (g * width + col0)
             scale0 = (PASSES * (mic - first) + g) * width + col0
             return (
                 codes4[name, mic][:, byte0 : byte0 + 2 * K_PASS].bitcast(FP4X4),
-                planes[name, first][:, scale0 : scale0 + K_PASS],
+                plane[:, scale0 : scale0 + K_PASS],
             )
 
         frames = {}
@@ -101,44 +102,42 @@ def tile_mic_spectrogram_magnitudes_b12_kernel(
             for j in range(count):
                 frames[first + j] = (raw, j)
 
-        spread = {}
-
-        def load_spread(name, rows, first, last):
-            width = rows.shape[1]
-            wide = sb.tile([P, (last - first) * width], BF16, name="%s_spread%d" % (name, first), align_bytes=64)
-            nc.sync.dma_start(out=wide[:], in_=rows[first:last].rearrange("g n -> (g n)").partition_broadcast(P))
-            for mic in range(first, last):
-                spread[name, mic] = (wide, (mic - first) * width)
-
         scale_rows = X_scale.rearrange("g (t p) b -> p (g t) b", p=P)
         x_scale_first = sb.tile([P, 1, L // Q], F32, name="x_scale_first")
         x_scale_rest = sb.tile([P, TILES - 1, L // Q], F32, name="x_scale_rest")
+        window_cols = sb.tile([P, G, L // P], BF16, name="window_cols")
+        gain_cols = sb.tile([P, G, F // P], BF16, name="gain_cols")
+
+        clear_plane("A", 0, 1)
+        clear_plane("C", 0, G)
+        clear_plane("S", 0, G)
         load_frames(0, 1)
         nc.sync.dma_start(out=x_scale_first[:], in_=scale_rows[:, 0:1, :])
-        load_frames(1, TILES_PER_MIC)
-        nc.sync.dma_start(out=x_scale_rest[:], in_=scale_rows[:, 1:TILES, :])
+        nc.sync.dma_start(out=window_cols[:], in_=window.rearrange("g (p c) -> p g c", p=P))
         load_scales("A", 0, 1)
         load_words("A", 0)
-        load_spread("window", window, 0, 1)
+        load_frames(1, TILES_PER_MIC)
+        nc.sync.dma_start(out=x_scale_rest[:], in_=scale_rows[:, 1:TILES, :])
+        nc.sync.dma_start(out=gain_cols[:], in_=gain.rearrange("g (p c) -> p g c", p=P))
         load_frames(TILES_PER_MIC, 2 * TILES_PER_MIC)
-        load_scales("C", 0, 1)
-        load_scales("S", 0, 1)
         load_words("C", 0)
         load_words("S", 0)
-        load_spread("gain", gain, 0, G)
-        load_scales("A", 1, G)
-        load_words("A", 1)
-        load_spread("window", window, 1, G)
-        load_scales("C", 1, G)
-        load_scales("S", 1, G)
-        load_words("C", 1)
-        load_words("S", 1)
-        for mic in range(2, G):
-            load_frames(mic * TILES_PER_MIC, (mic + 1) * TILES_PER_MIC)
-            for name in weights:
-                load_words(name, mic)
+        load_scales("C", 0, G)
+        load_scales("S", 0, G)
 
-        x_wide = [ring("x_wide%d_" % g, 4, [P, K_PASS], BF16) for g in range(PASSES)]
+        def load_later_mics():
+            clear_plane("A", 1, G)
+            load_scales("A", 1, G)
+            for mic in range(1, G):
+                load_words("A", mic)
+                if mic + 1 < G:
+                    load_frames((mic + 1) * TILES_PER_MIC, (mic + 2) * TILES_PER_MIC)
+                load_words("C", mic)
+                load_words("S", mic)
+
+        window_rows = ring("window_rows", G, [P, L], BF16)
+        gain_rows = ring("gain_rows", G // 2, [P, 2 * F], BF16)
+        x_wide = [ring("x_wide%d_" % g, 3, [P, K_PASS], BF16) for g in range(PASSES)]
         x_grouped = ring("x_grouped", 2, [P, L], BF16)
         x_codes = ring("x_codes", 2, [P, PASSES * P], U32)
         x_planes = ring("x_planes", 2, [P, PASSES * P], U8)
@@ -158,7 +157,7 @@ def tile_mic_spectrogram_magnitudes_b12_kernel(
 
         x_turned = ps.tile([P, 2 * PASSES * P], F32, name="x_turned")
         h_turned = [ps.tile([P, 2 * PASSES * P], F32, name="h_turned%d" % j) for j in range(2)]
-        y_turned = ps.tile([P, 2 * P], F32, name="y_turned")
+        y_turned = ps.tile([P, 4 * P], F32, name="y_turned")
         h_sum = [ps.tile([P, K_PASS], F32, name="h_sum%d" % g) for g in range(PASSES)]
         re_sum = ps.tile([P, F], F32, name="re_sum")
         im_sum = ps.tile([P, F], F32, name="im_sum")
@@ -175,22 +174,36 @@ def tile_mic_spectrogram_magnitudes_b12_kernel(
         def widen(i, g):
             raw, j = frames[i]
             row_scales = x_scale_first[:, 0, :] if i == 0 else x_scale_rest[:, i - 1, :]
+            target = slot(x_wide[g], i)[:].rearrange("p (u q e) -> p q u e", u=2, e=2)
             for b in range(BLOCKS_PER_PASS):
                 block = BLOCKS_PER_PASS * g + b
-                target = slot(x_wide[g], i)[:, Q * b : Q * (b + 1)]
-                codes = raw[:, j, Q * block : Q * (block + 1)].bitcast(FP8)
-                scale = row_scales[:, block : block + 1]
-                if (i, g) == (0, 1):
-                    nc.scalar.activation(out=target, in_=codes, func=ACT.Copy, scale=scale)
-                else:
-                    nc.vector.tensor_scalar(out=target, in0=codes, scalar1=scale, scalar2=None, op0=ALU.mult)
+                nc.vector.tensor_scalar(
+                    out=target[:, 32 * b : 32 * (b + 1), :, :],
+                    in0=raw[:, j, Q * block : Q * (block + 1)].bitcast(FP8).rearrange("p (q u e) -> p q u e", u=2, e=2),
+                    scalar1=row_scales[:, block : block + 1],
+                    scalar2=None,
+                    op0=ALU.mult,
+                )
 
-        def turn_frames(bank, halves):
-            for g, half in enumerate(halves):
-                words = half[:].bitcast(F32)
-                for u in range(2):
-                    col = (2 * g + u) * P
-                    nc.tensor.transpose(bank[:, col : col + P], words[:, u : 2 * P : 2], ident[:])
+        def spread_columns(bank, columns):
+            for n, column in enumerate(columns):
+                nc.tensor.transpose(bank[:, n * P : (n + 1) * P], column.to_broadcast([P, P]), ident[:])
+
+        def spread_window(mic, bank):
+            words = window_cols[:].bitcast(F32)
+            spread_columns(bank, [words[:, mic, c : c + 1] for c in range(4)])
+            nc.scalar.copy(
+                out=window_rows[mic][:].bitcast(F32).rearrange("p (g u l h) -> p g u l h", g=PASSES, u=2, h=2),
+                in_=bank[:].rearrange("p (h u g l) -> p g u l h", g=PASSES, u=2, h=2),
+            )
+
+        def spread_gain(pair, bank):
+            words = gain_cols[:].bitcast(F32)
+            spread_columns(bank, [words[:, 2 * pair + m, c : c + 1] for m in range(2) for c in range(2)])
+            nc.scalar.copy(
+                out=gain_rows[pair][:].bitcast(F32).rearrange("p (m j c) -> p m j c", m=2, c=2),
+                in_=bank[:].rearrange("p (m c j) -> p m j c", m=2, c=2),
+            )
 
         def turn(bank, halves):
             for g, half in enumerate(halves):
@@ -222,24 +235,22 @@ def tile_mic_spectrogram_magnitudes_b12_kernel(
                 )
 
         def apply_window(i, g):
-            wide, col0 = spread["window", i // TILES_PER_MIC]
-            col = col0 + g * K_PASS
             nc.vector.tensor_tensor(
                 out=sorted_pairs(slot(h_wide[g], i)[:]),
                 in0=by_pairs(h_sum[g][:]),
-                in1=by_pairs(wide[:, col : col + K_PASS]),
+                in1=sorted_pairs(window_rows[i // TILES_PER_MIC][:, g * K_PASS : (g + 1) * K_PASS]),
                 op=ALU.mult,
             )
 
         def apply_gain(i, cols=slice(0, F)):
-            wide, col0 = spread["gain", i // TILES_PER_MIC]
+            mic, t = divmod(i, TILES_PER_MIC)
+            col0 = (mic % 2) * F
             nc.vector.tensor_tensor(
                 out=slot(y_full, i)[:, cols],
                 in0=slot(magnitude, i)[:, cols],
-                in1=wide[:, col0 + cols.start : col0 + cols.stop],
+                in1=gain_rows[mic // 2][:, col0 + cols.start : col0 + cols.stop],
                 op=ALU.mult,
             )
-            mic, t = divmod(i, TILES_PER_MIC)
             nc.sync.dma_start(out=out_0[mic, P * t : P * (t + 1), cols], in_=slot(y_full, i)[:, cols])
 
         words_out = out_1[0].rearrange("p m t -> p (m t)").bitcast(I32)
@@ -281,9 +292,9 @@ def tile_mic_spectrogram_magnitudes_b12_kernel(
             turn(y_turned, [slot(y_half, i)])
 
         def group_y(copy, i):
-            group(copy, slot(y_grouped, i)[:], y_turned[:])
+            group(copy, slot(y_grouped, i)[:], y_turned[:, 0 : 2 * P])
 
-        for s in range(-3, TILES):
+        for s in range(-2, TILES):
             if live(s - 1):
                 turn(slot(h_turned, s - 1), h_halves(s - 1))
             if live(s - 2):
@@ -291,14 +302,16 @@ def tile_mic_spectrogram_magnitudes_b12_kernel(
             if live(s):
                 quantize(slot(x_codes, s)[:], slot(x_planes, s)[:], slot(x_grouped, s)[:])
             if live(s + 1):
-                turn_frames(x_turned, x_halves(s + 1))
+                turn(x_turned, x_halves(s + 1))
             if live(s - 5):
                 quantize_y(s - 5)
             if live(s - 4):
                 turn_y(s - 4)
-            if live(s + 3):
-                widen(s + 3, 0)
-                widen(s + 3, 1)
+            if live(s + 2):
+                widen(s + 2, 0)
+                widen(s + 2, 1)
+            if s == -2:
+                load_later_mics()
             if live(s - 1):
                 group(nc.scalar.copy, slot(h_grouped, s - 1)[:], slot(h_turned, s - 1)[:])
             if live(s - 2):
@@ -308,6 +321,15 @@ def tile_mic_spectrogram_magnitudes_b12_kernel(
                     multiply(h_sum[g], slot(x_codes, s), slot(x_planes, s), "A", s, g * K_PASS)
             if live(s + 1):
                 group(nc.scalar.copy, slot(x_grouped, s + 1)[:], x_turned[:])
+            if s == -2:
+                spread_window(0, re_sum)
+            if s == -1:
+                spread_window(1, im_sum)
+                spread_window(2, y_turned)
+            if s == 0:
+                spread_window(3, h_turned[1])
+                spread_gain(0, re_sum)
+                spread_gain(1, im_sum)
             if live(s - 1):
                 quantize(slot(h_codes, s - 1)[:], slot(h_planes, s - 1)[:], slot(h_grouped, s - 1)[:])
             if live(s - 4):

@@ -18,13 +18,15 @@ ACT = mybir.ActivationFunctionType
 ALU = mybir.AluOpType
 
 P = 128
+BANK = 512
 K_PASS = 512
 PASSES = L // K_PASS
 TILES_PER_MIC = T // P
 TILES = G * TILES_PER_MIC
 BLOCKS_PER_PASS = K_PASS // Q
-ROUND_ON_VECTOR_FROM = 7
-STORE_AFTER = {2: 0, 5: 3, 8: 6, 10: 9, 11: 11}
+QUADS = 4
+WIDEN_AHEAD = 5
+FIRST_STEP = 3
 
 
 def tile_mic_spectrogram_magnitudes_b12_kernel(
@@ -39,6 +41,9 @@ def tile_mic_spectrogram_magnitudes_b12_kernel(
         def ring(name, depth, shape, dtype):
             return [sb.tile(shape, dtype, name="%s%d" % (name, j), align_bytes=64) for j in range(depth)]
 
+        def slot(tiles, i):
+            return tiles[i % len(tiles)]
+
         ident = sb.tile([P, P], F32, name="ident")
         make_identity(nc, ident[:])
 
@@ -48,365 +53,411 @@ def tile_mic_spectrogram_magnitudes_b12_kernel(
         nc.scalar.activation(out=warm_out[:], in_=warm[:], func=ACT.Sqrt)
 
         weights = {"A": (A_words, A_scales, L), "C": (C_words, C_scales, F), "S": (S_words, S_scales, F)}
-        planes = {}
+        weight_scales = {}
+        weight_words = {}
 
-        def clear_plane(name, first, last):
+        def clear_scales(name, first, last):
             width = weights[name][2]
-            plane = sb.tile([P, (last - first) * PASSES * width], U8, name="%s_plane%d" % (name, first), align_bytes=64)
-            nc.vector.memset(plane[:].bitcast(I32), 0)
+            rows = sb.tile([P, (last - first) * PASSES * width], U8, name="%s_scales%d" % (name, first), align_bytes=64)
+            nc.vector.memset(rows[:].bitcast(I32), 0)
             for mic in range(first, last):
-                planes[name, mic] = (plane, first)
+                weight_scales[name, mic] = (rows, first)
 
         def load_scales(name, first, last):
             scales, width = weights[name][1:]
-            plane = planes[name, first][0]
-            for quad in range(4):
+            rows = weight_scales[name, first][0]
+            for quad in range(QUADS):
                 nc.sync.dma_start(
-                    out=plane[32 * quad : 32 * quad + 4, :].bitcast(I32).rearrange("r (g n) -> r g n", n=width // 4),
+                    out=rows[32 * quad : 32 * quad + 4, :].bitcast(I32).rearrange("r (g n) -> r g n", n=width // 4),
                     in_=scales[PASSES * first : PASSES * last, 4 * quad : 4 * quad + 4, :]
                     .bitcast(I32)
                     .rearrange("g r n -> r g n"),
                 )
 
-        codes4 = {}
-
         def load_words(name, mic):
-            words, scales, width = weights[name]
-            tile4 = sb.tile([P, PASSES * 2 * width], U8, name="%s_words%d" % (name, mic), align_bytes=64)
+            words, width = weights[name][0], weights[name][2]
+            packed = sb.tile([P, PASSES * 2 * width], U8, name="%s_words%d" % (name, mic), align_bytes=64)
             nc.sync.dma_start(
-                out=tile4[:].bitcast(I32).rearrange("p (g n) -> p g n", g=PASSES),
+                out=packed[:].bitcast(I32).rearrange("p (g n) -> p g n", g=PASSES),
                 in_=words[PASSES * mic : PASSES * (mic + 1)].bitcast(I32).rearrange("g p n -> p g n"),
             )
-            codes4[name, mic] = tile4
+            weight_words[name, mic] = packed
 
-        def weight_operand(name, mic, g, col0):
-            width = weights[name][2]
-            plane, first = planes[name, mic]
-            byte0 = 2 * (g * width + col0)
-            scale0 = (PASSES * (mic - first) + g) * width + col0
-            return (
-                codes4[name, mic][:, byte0 : byte0 + 2 * K_PASS].bitcast(FP4X4),
-                plane[:, scale0 : scale0 + K_PASS],
-            )
-
-        frames = {}
+        frame_bytes = {}
+        frame_scales = {}
+        byte_rows = X_bytes.rearrange("g (t p) k -> p (g t) k", p=P)
+        scale_rows = X_scale.rearrange("g (t p) b -> p (g t) b", p=P)
 
         def load_frames(first, last):
-            mic, t0 = divmod(first, TILES_PER_MIC)
-            count = last - first
-            raw = sb.tile([P, count, L], U8, name="frame_bytes%d" % first, align_bytes=64)
-            nc.sync.dma_start(
-                out=raw[:],
-                in_=X_bytes[mic, P * t0 : P * (t0 + count), :].rearrange("(t p) k -> p t k", p=P),
-            )
-            for j in range(count):
-                frames[first + j] = (raw, j)
+            raw = sb.tile([P, last - first, L], U8, name="frame_bytes%d" % first, align_bytes=64)
+            nc.sync.dma_start(out=raw[:], in_=byte_rows[:, first:last, :])
+            for i in range(first, last):
+                frame_bytes[i] = raw[:, i - first, :]
 
-        scale_rows = X_scale.rearrange("g (t p) b -> p (g t) b", p=P)
-        x_scale_first = sb.tile([P, 1, L // Q], F32, name="x_scale_first")
-        x_scale_rest = sb.tile([P, TILES - 1, L // Q], F32, name="x_scale_rest")
+        def load_frame_scales(first, last):
+            scales = sb.tile([P, last - first, L // Q], F32, name="frame_scales%d" % first)
+            nc.sync.dma_start(out=scales[:], in_=scale_rows[:, first:last, :])
+            for i in range(first, last):
+                frame_scales[i] = scales[:, i - first, :]
+
         window_cols = sb.tile([P, G, L // P], BF16, name="window_cols")
         gain_cols = sb.tile([P, G, F // P], BF16, name="gain_cols")
 
-        clear_plane("A", 0, 1)
-        clear_plane("C", 0, G)
-        clear_plane("S", 0, G)
+        clear_scales("A", 0, 1)
+        clear_scales("C", 0, G)
+        clear_scales("S", 0, G)
         load_frames(0, 1)
-        nc.sync.dma_start(out=x_scale_first[:], in_=scale_rows[:, 0:1, :])
+        load_frame_scales(0, TILES_PER_MIC)
+        load_frames(1, TILES_PER_MIC)
         nc.sync.dma_start(out=window_cols[:], in_=window.rearrange("g (p c) -> p g c", p=P))
         load_scales("A", 0, 1)
         load_words("A", 0)
-        load_frames(1, TILES_PER_MIC)
-        nc.sync.dma_start(out=x_scale_rest[:], in_=scale_rows[:, 1:TILES, :])
-        nc.sync.dma_start(out=gain_cols[:], in_=gain.rearrange("g (p c) -> p g c", p=P))
+        load_frame_scales(TILES_PER_MIC, TILES)
         load_frames(TILES_PER_MIC, 2 * TILES_PER_MIC)
+        nc.sync.dma_start(out=gain_cols[:], in_=gain.rearrange("g (p c) -> p g c", p=P))
+        load_frames(2 * TILES_PER_MIC, TILES)
         load_words("C", 0)
         load_words("S", 0)
         load_scales("C", 0, G)
         load_scales("S", 0, G)
 
-        def load_later_mics():
-            clear_plane("A", 1, G)
+        def load_later_weights():
+            clear_scales("A", 1, G)
             load_scales("A", 1, G)
             for mic in range(1, G):
-                load_words("A", mic)
-                if mic + 1 < G:
-                    load_frames((mic + 1) * TILES_PER_MIC, (mic + 2) * TILES_PER_MIC)
-                load_words("C", mic)
-                load_words("S", mic)
+                for name in weights:
+                    load_words(name, mic)
 
         window_rows = ring("window_rows", G, [P, L], BF16)
         gain_rows = ring("gain_rows", G // 2, [P, 2 * F], BF16)
-        x_wide = [ring("x_wide%d_" % g, 3, [P, K_PASS], BF16) for g in range(PASSES)]
-        x_grouped = ring("x_grouped", 2, [P, L], BF16)
-        x_codes = ring("x_codes", 2, [P, PASSES * P], U32)
-        x_planes = ring("x_planes", 2, [P, PASSES * P], U8)
-        h_wide = [ring("h_wide%d_" % g, 2, [P, K_PASS], BF16) for g in range(PASSES)]
-        h_grouped = ring("h_grouped", 2, [P, L], BF16)
-        h_codes = ring("h_codes", 2, [P, PASSES * P], U32)
-        h_planes = ring("h_planes", 2, [P, PASSES * P], U8)
-        re_sq = ring("re_sq", 2, [P, F], F32)
-        im_sq = ring("im_sq", 2, [P, F], F32)
-        power = ring("power", 2, [P, F], F32)
-        magnitude = ring("magnitude", 2, [P, F], F32)
+        x_pairs = [ring("x_pairs%d_" % g, WIDEN_AHEAD, [P, K_PASS], BF16) for g in range(PASSES)]
+        x_quads = ring("x_quads", 3, [P, L], BF16)
+        x_codes = ring("x_codes", 3, [P, PASSES * P], U32)
+        x_scales = ring("x_scales", 3, [P, PASSES * P], U8)
+        h_pairs = [ring("h_pairs%d_" % g, 3, [P, K_PASS], BF16) for g in range(PASSES)]
+        h_quads = ring("h_quads", 3, [P, L], BF16)
+        h_codes = ring("h_codes", 3, [P, PASSES * P], U32)
+        h_scales = ring("h_scales", 3, [P, PASSES * P], U8)
+        re_sq = ring("re_sq", 3, [P, F], F32)
+        im_sq = ring("im_sq", 3, [P, F], F32)
+        power = ring("power", 3, [P, F], F32)
+        magnitude = ring("magnitude", 3, [P, F], F32)
         y_full = ring("y_full", 4, [P, F], F32)
-        y_half = ring("y_half", 2, [P, F], BF16)
-        y_grouped = ring("y_grouped", 2, [P, F], BF16)
+        y_pairs = ring("y_pairs", 3, [P, F], BF16)
+        y_quads = ring("y_quads", 3, [P, F], BF16)
         y_codes = sb.tile([P, TILES * P], U32, name="y_codes", align_bytes=64)
-        y_plane = sb.tile([P, TILES * P], U8, name="y_plane", align_bytes=64)
+        y_scales = sb.tile([P, TILES * P], U8, name="y_scales", align_bytes=64)
 
-        x_turned = ps.tile([P, 2 * PASSES * P], F32, name="x_turned")
-        h_turned = [ps.tile([P, 2 * PASSES * P], F32, name="h_turned%d" % j) for j in range(2)]
-        y_turned = ps.tile([P, 4 * P], F32, name="y_turned")
-        h_sum = [ps.tile([P, K_PASS], F32, name="h_sum%d" % g) for g in range(PASSES)]
-        re_sum = ps.tile([P, F], F32, name="re_sum")
-        im_sum = ps.tile([P, F], F32, name="im_sum")
+        x_bank = ps.tile([P, BANK], F32, name="x_bank")
+        h_banks = [ps.tile([P, BANK], F32, name="h_bank%d" % j) for j in range(2)]
+        y_bank = ps.tile([P, BANK], F32, name="y_bank")
+        a_banks = [ps.tile([P, BANK], F32, name="a_bank%d" % j) for j in range(2)]
+        spec_banks = [ps.tile([P, BANK], F32, name="spec_bank%d" % j) for j in range(2)]
 
-        def slot(tiles, i):
-            return tiles[i % len(tiles)]
-
-        def by_pairs(ap):
+        def in_k_order(ap):
             return ap.rearrange("p (q u e) -> p u q e", u=2, e=2)
 
-        def sorted_pairs(ap):
+        def in_pair_order(ap):
             return ap.rearrange("p (u q e) -> p u q e", u=2, e=2)
 
-        def widen(i, g):
-            raw, j = frames[i]
-            row_scales = x_scale_first[:, 0, :] if i == 0 else x_scale_rest[:, i - 1, :]
-            target = slot(x_wide[g], i)[:].rearrange("p (u q e) -> p q u e", u=2, e=2)
-            for b in range(BLOCKS_PER_PASS):
-                block = BLOCKS_PER_PASS * g + b
-                nc.vector.tensor_scalar(
-                    out=target[:, 32 * b : 32 * (b + 1), :, :],
-                    in0=raw[:, j, Q * block : Q * (block + 1)].bitcast(FP8).rearrange("p (q u e) -> p q u e", u=2, e=2),
-                    scalar1=row_scales[:, block : block + 1],
-                    scalar2=None,
-                    op0=ALU.mult,
+        def turn(bank, halves):
+            for g, half in enumerate(halves):
+                pairs = half[:].bitcast(F32)
+                for u in range(2):
+                    col = (2 * g + u) * P
+                    nc.tensor.transpose(bank[:, col : col + P], pairs[:, u * P : (u + 1) * P], ident[:])
+
+        def join(copy, quads, turned):
+            copy(
+                out=quads.bitcast(F32).rearrange("p (g r u) -> p g r u", r=P, u=2),
+                in_=turned.rearrange("p (g u r) -> p g r u", r=P, u=2),
+            )
+
+        def quantize(codes, scales, quads):
+            nc.vector.quantize_mx(out=codes.bitcast(FP8X4), scales=scales, in_=quads)
+
+        def multiply(bank, codes, scales, name, i, col0, passes):
+            mic = i // TILES_PER_MIC
+            width = weights[name][2]
+            rows, first = weight_scales[name, mic]
+            for g in passes:
+                byte0 = 2 * (g * width + col0)
+                scale0 = (PASSES * (mic - first) + g) * width + col0
+                nc.tensor.matmul_mx(
+                    out=bank[:],
+                    lhsT=codes[:, g * P : (g + 1) * P].bitcast(FP8X4),
+                    lhsT_scale=scales[:, g * P : (g + 1) * P],
+                    rhs=weight_words[name, mic][:, byte0 : byte0 + 2 * BANK].bitcast(FP4X4),
+                    rhs_scale=rows[:, scale0 : scale0 + BANK],
+                    start=(g == 0),
+                    stop=(g == PASSES - 1),
                 )
 
-        def spread_columns(bank, columns):
+        def spread(bank, columns):
             for n, column in enumerate(columns):
                 nc.tensor.transpose(bank[:, n * P : (n + 1) * P], column.to_broadcast([P, P]), ident[:])
 
         def spread_window(mic, bank):
-            words = window_cols[:].bitcast(F32)
-            spread_columns(bank, [words[:, mic, c : c + 1] for c in range(4)])
+            pairs = window_cols[:].bitcast(F32)
+            spread(bank, [pairs[:, mic, c : c + 1] for c in range(4)])
+
+        def keep_window(mic, bank):
             nc.scalar.copy(
                 out=window_rows[mic][:].bitcast(F32).rearrange("p (g u l h) -> p g u l h", g=PASSES, u=2, h=2),
                 in_=bank[:].rearrange("p (h u g l) -> p g u l h", g=PASSES, u=2, h=2),
             )
 
-        def spread_gain(pair, bank):
-            words = gain_cols[:].bitcast(F32)
-            spread_columns(bank, [words[:, 2 * pair + m, c : c + 1] for m in range(2) for c in range(2)])
+        def spread_gain(half, bank):
+            pairs = gain_cols[:].bitcast(F32)
+            spread(bank, [pairs[:, 2 * half + m, c : c + 1] for m in range(2) for c in range(2)])
+
+        def keep_gain(half, bank):
             nc.scalar.copy(
-                out=gain_rows[pair][:].bitcast(F32).rearrange("p (m j c) -> p m j c", m=2, c=2),
+                out=gain_rows[half][:].bitcast(F32).rearrange("p (m j c) -> p m j c", m=2, c=2),
                 in_=bank[:].rearrange("p (m c j) -> p m j c", m=2, c=2),
             )
 
-        def turn(bank, halves):
-            for g, half in enumerate(halves):
-                words = half[:].bitcast(F32)
-                for u in range(2):
-                    col = (2 * g + u) * P
-                    nc.tensor.transpose(bank[:, col : col + P], words[:, u * P : (u + 1) * P], ident[:])
+        def widen(i):
+            for g in range(PASSES):
+                target = slot(x_pairs[g], i)[:].rearrange("p (u q e) -> p q u e", u=2, e=2)
+                for b in range(BLOCKS_PER_PASS):
+                    block = BLOCKS_PER_PASS * g + b
+                    codes = frame_bytes[i][:, Q * block : Q * (block + 1)].bitcast(FP8)
+                    nc.vector.tensor_scalar(
+                        out=target[:, (Q // 4) * b : (Q // 4) * (b + 1), :, :],
+                        in0=codes.rearrange("p (q u e) -> p q u e", u=2, e=2),
+                        scalar1=frame_scales[i][:, block : block + 1],
+                        scalar2=None,
+                        op0=ALU.mult,
+                    )
 
-        def group(copy, grouped, bank):
-            copy(
-                out=grouped.bitcast(F32).rearrange("p (g r u) -> p g r u", r=P, u=2),
-                in_=bank.rearrange("p (g u r) -> p g r u", r=P, u=2),
-            )
+        def turn_x(i, bank=x_bank):
+            turn(bank, [slot(x_pairs[g], i) for g in range(PASSES)])
 
-        def quantize(codes, plane, grouped):
-            nc.vector.quantize_mx(out=codes.bitcast(FP8X4), scales=plane, in_=grouped)
+        def join_x(i, bank=x_bank):
+            join(nc.scalar.copy, slot(x_quads, i)[:], bank[:])
 
-        def multiply(acc, codes, plane, name, i, col0, passes=range(PASSES)):
-            for g in passes:
-                rhs, rhs_scale = weight_operand(name, i // TILES_PER_MIC, g, col0)
-                nc.tensor.matmul_mx(
-                    out=acc[:],
-                    lhsT=codes[:, g * P : (g + 1) * P].bitcast(FP8X4),
-                    lhsT_scale=plane[:, g * P : (g + 1) * P],
-                    rhs=rhs,
-                    rhs_scale=rhs_scale,
-                    start=(g == 0),
-                    stop=(g == PASSES - 1),
-                )
+        def quantize_x(i):
+            quantize(slot(x_codes, i)[:], slot(x_scales, i)[:], slot(x_quads, i)[:])
 
-        def apply_window(i, g):
+        def correct(i, banks=a_banks):
+            for n, bank in enumerate(banks):
+                multiply(bank, slot(x_codes, i), slot(x_scales, i), "A", i, n * BANK, range(PASSES))
+
+        def apply_window(i, g, banks=a_banks):
             nc.vector.tensor_tensor(
-                out=sorted_pairs(slot(h_wide[g], i)[:]),
-                in0=by_pairs(h_sum[g][:]),
-                in1=sorted_pairs(window_rows[i // TILES_PER_MIC][:, g * K_PASS : (g + 1) * K_PASS]),
+                out=in_pair_order(slot(h_pairs[g], i)[:]),
+                in0=in_k_order(banks[g][:]),
+                in1=in_pair_order(window_rows[i // TILES_PER_MIC][:, g * K_PASS : (g + 1) * K_PASS]),
                 op=ALU.mult,
             )
 
-        def apply_gain(i, cols=slice(0, F)):
+        def turn_h(i):
+            turn(slot(h_banks, i), [slot(h_pairs[g], i) for g in range(PASSES)])
+
+        def join_h(i):
+            join(nc.scalar.copy, slot(h_quads, i)[:], slot(h_banks, i)[:])
+
+        def quantize_h(i):
+            quantize(slot(h_codes, i)[:], slot(h_scales, i)[:], slot(h_quads, i)[:])
+
+        def transform(i, banks=spec_banks, passes=range(PASSES)):
+            for bank, name in zip(banks, ("C", "S")):
+                multiply(bank, slot(h_codes, i), slot(h_scales, i), name, i, 0, passes)
+
+        def square_re(i, banks=spec_banks):
+            nc.scalar.activation(out=slot(re_sq, i)[:], in_=banks[0][:], func=ACT.Square)
+
+        def square_im(i, banks=spec_banks):
+            nc.scalar.activation(out=slot(im_sq, i)[:], in_=banks[1][:], func=ACT.Square)
+
+        def add_squares(i):
+            nc.vector.tensor_tensor(out=slot(power, i)[:], in0=slot(re_sq, i)[:], in1=slot(im_sq, i)[:], op=ALU.add)
+
+        def root(i):
+            nc.scalar.activation(out=slot(magnitude, i)[:], in_=slot(power, i)[:], func=ACT.Sqrt)
+
+        def apply_gain(i):
             mic, t = divmod(i, TILES_PER_MIC)
             col0 = (mic % 2) * F
             nc.vector.tensor_tensor(
-                out=slot(y_full, i)[:, cols],
-                in0=slot(magnitude, i)[:, cols],
-                in1=gain_rows[mic // 2][:, col0 + cols.start : col0 + cols.stop],
-                op=ALU.mult,
+                out=slot(y_full, i)[:], in0=slot(magnitude, i)[:], in1=gain_rows[mic // 2][:, col0 : col0 + F], op=ALU.mult
             )
-            nc.sync.dma_start(out=out_0[mic, P * t : P * (t + 1), cols], in_=slot(y_full, i)[:, cols])
+            nc.sync.dma_start(out=out_0[mic, P * t : P * (t + 1), :], in_=slot(y_full, i)[:])
 
-        words_out = out_1[0].rearrange("p m t -> p (m t)").bitcast(I32)
+        def round_y(i, copy):
+            copy(out=in_pair_order(slot(y_pairs, i)[:]), in_=in_k_order(slot(y_full, i)[:]))
+
+        def turn_y(i, bank=y_bank):
+            turn(bank, [slot(y_pairs, i)])
+
+        def join_y(i, copy, bank=y_bank):
+            join(copy, slot(y_quads, i)[:], bank[:, 0 : 2 * P])
+
+        code_rows = out_1[0].rearrange("p m t -> p (m t)").bitcast(I32)
 
         def store_codes(first, last):
-            nc.sync.dma_start(out=words_out[:, P * first : P * last], in_=y_codes[:, P * first : P * last].bitcast(I32))
-
-        def live(i):
-            return 0 <= i < TILES
-
-        def x_halves(i):
-            return [slot(x_wide[g], i) for g in range(PASSES)]
-
-        def h_halves(i):
-            return [slot(h_wide[g], i) for g in range(PASSES)]
-
-        def round_y(i, cols=slice(0, F)):
-            copy = nc.vector.tensor_copy if i >= ROUND_ON_VECTOR_FROM else nc.scalar.copy
-            quads = slice(cols.start // 4, cols.stop // 4)
-            copy(out=sorted_pairs(slot(y_half, i)[:])[:, :, quads, :], in_=by_pairs(slot(y_full, i)[:, cols]))
+            nc.sync.dma_start(out=code_rows[:, P * first : P * last], in_=y_codes[:, P * first : P * last].bitcast(I32))
 
         def quantize_y(i):
-            quantize(y_codes[:, P * i : P * (i + 1)], y_plane[:, P * i : P * (i + 1)], slot(y_grouped, i)[:])
-            if i in STORE_AFTER:
-                store_codes(STORE_AFTER[i], i + 1)
+            quantize(y_codes[:, P * i : P * (i + 1)], y_scales[:, P * i : P * (i + 1)], slot(y_quads, i)[:])
+            if i < TILES - TILES_PER_MIC and (i + 1) % TILES_PER_MIC == 0:
+                store_codes(i + 1 - TILES_PER_MIC, i + 1)
 
-        def square(squares, sums, i, cols=slice(0, F)):
-            nc.scalar.activation(out=slot(squares, i)[:, cols], in_=sums[:, cols], func=ACT.Square)
+        on_scalar, on_vector = nc.scalar.copy, nc.vector.tensor_copy
 
-        def add_squares(i, cols=slice(0, F)):
-            nc.vector.tensor_tensor(
-                out=slot(power, i)[:, cols], in0=slot(re_sq, i)[:, cols], in1=slot(im_sq, i)[:, cols], op=ALU.add
-            )
+        widen(0)
+        spread_window(0, spec_banks[0])
+        keep_window(0, spec_banks[0])
+        turn_x(0)
+        widen(1)
+        join_x(0)
+        turn_x(1, h_banks[0])
+        widen(2)
+        load_later_weights()
+        join_x(1, h_banks[0])
+        turn_x(2, h_banks[1])
+        quantize_x(0)
+        spread_window(1, spec_banks[1])
+        join_x(2, h_banks[1])
+        keep_window(1, spec_banks[1])
+        widen(3)
+        quantize_x(1)
+        quantize_x(2)
+        correct(0)
+        correct(1, spec_banks)
+        widen(4)
+        widen(5)
+        apply_window(0, 0)
+        apply_window(0, 1)
+        turn_x(3)
+        spread_gain(0, y_bank)
+        turn_h(0)
+        join_x(3)
+        apply_window(1, 0, spec_banks)
+        apply_window(1, 1, spec_banks)
+        widen(6)
+        join_h(0)
+        keep_gain(0, y_bank)
+        correct(2)
+        quantize_h(0)
+        quantize_x(3)
+        turn_h(1)
+        spread_window(2, h_banks[0])
+        apply_window(2, 0)
+        apply_window(2, 1)
+        widen(7)
+        transform(0)
+        join_h(1)
+        keep_window(2, h_banks[0])
+        square_re(0)
 
-        def root(i, cols=slice(0, F)):
-            nc.scalar.activation(out=slot(magnitude, i)[:, cols], in_=slot(power, i)[:, cols], func=ACT.Sqrt)
-
-        def turn_y(i):
-            turn(y_turned, [slot(y_half, i)])
-
-        def group_y(copy, i):
-            group(copy, slot(y_grouped, i)[:], y_turned[:, 0 : 2 * P])
-
-        for s in range(-2, TILES):
-            if live(s - 1):
-                turn(slot(h_turned, s - 1), h_halves(s - 1))
-            if live(s - 2):
-                square(im_sq, im_sum, s - 2)
-            if live(s):
-                quantize(slot(x_codes, s)[:], slot(x_planes, s)[:], slot(x_grouped, s)[:])
-            if live(s + 1):
-                turn(x_turned, x_halves(s + 1))
-            if live(s - 5):
-                quantize_y(s - 5)
-            if live(s - 4):
-                turn_y(s - 4)
-            if live(s + 2):
-                widen(s + 2, 0)
-                widen(s + 2, 1)
-            if s == -2:
-                load_later_mics()
-            if live(s - 1):
-                group(nc.scalar.copy, slot(h_grouped, s - 1)[:], slot(h_turned, s - 1)[:])
-            if live(s - 2):
-                add_squares(s - 2)
-            if live(s):
-                for g in range(PASSES):
-                    multiply(h_sum[g], slot(x_codes, s), slot(x_planes, s), "A", s, g * K_PASS)
-            if live(s + 1):
-                group(nc.scalar.copy, slot(x_grouped, s + 1)[:], x_turned[:])
-            if s == -2:
-                spread_window(0, re_sum)
-            if s == -1:
-                spread_window(1, im_sum)
-                spread_window(2, y_turned)
-            if s == 0:
-                spread_window(3, h_turned[1])
-                spread_gain(0, re_sum)
-                spread_gain(1, im_sum)
-            if live(s - 1):
-                quantize(slot(h_codes, s - 1)[:], slot(h_planes, s - 1)[:], slot(h_grouped, s - 1)[:])
-            if live(s - 4):
-                group_y(nc.scalar.copy, s - 4)
-            if live(s):
-                apply_window(s, 0)
-            if live(s - 1):
-                multiply(re_sum, slot(h_codes, s - 1), slot(h_planes, s - 1), "C", s - 1, 0)
-                multiply(im_sum, slot(h_codes, s - 1), slot(h_planes, s - 1), "S", s - 1, 0)
-            if live(s - 2):
-                root(s - 2)
-            if live(s):
-                apply_window(s, 1)
-            if live(s - 3):
-                round_y(s - 3)
-            if live(s - 2):
-                apply_gain(s - 2)
-            if live(s - 1):
-                square(re_sq, re_sum, s - 1)
-
+        late_spreads = {
+            FIRST_STEP: (spread_window, keep_window, G - 1),
+            FIRST_STEP + 1: (spread_gain, keep_gain, 1),
+        }
         last = TILES - 1
-        banks = [slot(h_turned, last), x_turned]
-        low, high = slice(0, F // 2), slice(F // 2, F)
+        for s in range(FIRST_STEP, TILES):
+            widening = s + WIDEN_AHEAD <= last
+            if s < last:
+                turn_x(s + 1)
+            if s >= 5:
+                turn_y(s - 5)
+            if s in late_spreads:
+                late_spreads[s][0](late_spreads[s][2], y_bank)
+            turn_h(s - 1)
+            square_im(s - 3)
+            quantize_h(s - 2)
+            if s < last:
+                join_x(s + 1)
+            if widening:
+                widen(s + WIDEN_AHEAD)
+            correct(s)
+            add_squares(s - 3)
+            if s >= 5:
+                join_y(s - 5, on_scalar)
+            if s in late_spreads:
+                late_spreads[s][1](late_spreads[s][2], y_bank)
+            join_h(s - 1)
+            if s < last:
+                quantize_x(s + 1)
+            apply_window(s, 0)
+            transform(s - 2)
+            root(s - 3)
+            apply_window(s, 1)
+            if s < last:
+                if s >= 4:
+                    round_y(s - 4, on_scalar if widening else on_vector)
+                if s >= 5:
+                    quantize_y(s - 5)
+                apply_gain(s - 3)
+                square_re(s - 2)
 
-        def group_last(g):
-            group(nc.scalar.copy, slot(h_grouped, last)[:, g * K_PASS : (g + 1) * K_PASS], banks[g][:, 0 : 2 * P])
+        pass_banks = [slot(h_banks, last), x_bank]
+
+        def join_last(g):
+            join(on_scalar, slot(h_quads, last)[:, g * K_PASS : (g + 1) * K_PASS], pass_banks[g][:, 0 : 2 * P])
 
         def quantize_last(g):
             quantize(
                 slot(h_codes, last)[:, g * P : (g + 1) * P],
-                slot(h_planes, last)[:, g * P : (g + 1) * P],
-                slot(h_grouped, last)[:, g * K_PASS : (g + 1) * K_PASS],
+                slot(h_scales, last)[:, g * P : (g + 1) * P],
+                slot(h_quads, last)[:, g * K_PASS : (g + 1) * K_PASS],
             )
 
+        quantize_h(last - 1)
         for g in range(PASSES):
-            turn(banks[g], [slot(h_wide[g], last)])
-        square(im_sq, im_sum, last - 1)
-        quantize_y(last - 4)
-        turn_y(last - 3)
-        group_last(0)
-        add_squares(last - 1)
-        group_last(1)
+            turn(pass_banks[g], [slot(h_pairs[g], last)])
+        square_re(last - 2)
+        round_y(last - 4, on_vector)
+        square_im(last - 2)
+        transform(last - 1)
+        join_last(0)
+        join_last(1)
+        apply_gain(last - 3)
+        quantize_y(last - 5)
+        add_squares(last - 2)
         quantize_last(0)
-        round_y(last - 2)
         quantize_last(1)
+        turn_y(last - 4)
         for g in range(PASSES):
-            multiply(re_sum, slot(h_codes, last), slot(h_planes, last), "C", last, 0, [g])
-            multiply(im_sum, slot(h_codes, last), slot(h_planes, last), "S", last, 0, [g])
+            transform(last, a_banks, [g])
+        square_re(last - 1)
+        round_y(last - 3, on_vector)
+        square_im(last - 1)
+        join_y(last - 4, on_vector)
+        root(last - 2)
+        turn_y(last - 3)
+        add_squares(last - 1)
+        quantize_y(last - 4)
+        square_re(last, a_banks)
+        apply_gain(last - 2)
+        square_im(last, a_banks)
+        join_y(last - 3, on_vector)
         root(last - 1)
-        group_y(nc.scalar.copy, last - 3)
+        round_y(last - 2, on_vector)
+        add_squares(last)
         turn_y(last - 2)
-        apply_gain(last - 1)
-        for cols in (low, high):
-            square(re_sq, re_sum, last, cols)
-            square(im_sq, im_sum, last, cols)
         quantize_y(last - 3)
-        group_y(nc.vector.tensor_copy, last - 2)
-        add_squares(last, low)
-        round_y(last - 1)
-        add_squares(last, high)
-        root(last, low)
-        root(last, high)
-        turn_y(last - 1)
+        apply_gain(last - 1)
+        root(last)
+        join_y(last - 2, on_scalar)
+        round_y(last - 1, on_vector)
+        apply_gain(last)
+        turn_y(last - 1, x_bank)
         quantize_y(last - 2)
-        apply_gain(last, low)
-        group_y(nc.scalar.copy, last - 1)
-        apply_gain(last, high)
-        round_y(last, low)
-        round_y(last, high)
+        round_y(last, on_vector)
+        join_y(last - 1, on_scalar, x_bank)
         turn_y(last)
         quantize_y(last - 1)
-        group_y(nc.vector.tensor_copy, last)
+        store_codes(TILES - TILES_PER_MIC, last)
+        join_y(last, on_vector)
         quantize_y(last)
+        store_codes(last, TILES)
 
-        for quad in range(4):
+        for quad in range(QUADS):
             queue = nc.scalar if quad % 2 == 0 else nc.sync
             queue.dma_start(
                 out=out_2[0, 4 * quad : 4 * quad + 4, :].bitcast(I32),
-                in_=y_plane[32 * quad : 32 * quad + 4, :].bitcast(I32),
+                in_=y_scales[32 * quad : 32 * quad + 4, :].bitcast(I32),
             )

from contextlib import ExitStack

import concourse.mybir as mybir
from concourse.masks import make_identity

G, T, L, F, Q = 4, 384, 1024, 512, 128
FLOPS = 2 * G * T * L * (L + 2 * F)

F32 = mybir.dt.float32
BF16 = mybir.dt.bfloat16
I32 = mybir.dt.int32
U32 = mybir.dt.uint32
U8 = mybir.dt.uint8
FP8 = mybir.dt.float8_e4m3fn
FP8X4 = mybir.dt.float8_e4m3fn_x4
FP4X4 = mybir.dt.float4_e2m1fn_x4
ACT = mybir.ActivationFunctionType
ALU = mybir.AluOpType

P = 128
BANK = 512
K_PASS = 512
PASSES = L // K_PASS
TILES_PER_MIC = T // P
TILES = G * TILES_PER_MIC
BLOCKS_PER_PASS = K_PASS // Q
QUADS = 4
WIDEN_AHEAD = 5
FIRST_STEP = 3


def tile_mic_spectrogram_magnitudes_b12_kernel(
    tc, X_bytes, X_scale, A_words, A_scales, C_words, C_scales, S_words, S_scales, window, gain, out_0, out_1, out_2
):
    nc = tc.nc
    with ExitStack() as ctx:
        sb = ctx.enter_context(tc.tile_pool(name="sb", bufs=1))
        ps = ctx.enter_context(tc.psum_pool(name="ps", bufs=1))
        ctx.enter_context(tc.manual_schedule())

        def ring(name, depth, shape, dtype):
            return [sb.tile(shape, dtype, name="%s%d" % (name, j), align_bytes=64) for j in range(depth)]

        def slot(tiles, i):
            return tiles[i % len(tiles)]

        ident = sb.tile([P, P], F32, name="ident")
        make_identity(nc, ident[:])

        warm = sb.tile([P, 8], F32, name="warm")
        warm_out = sb.tile([P, 8], F32, name="warm_out")
        nc.vector.memset(warm[:], 1.0)
        nc.scalar.activation(out=warm_out[:], in_=warm[:], func=ACT.Sqrt)

        weights = {"A": (A_words, A_scales, L), "C": (C_words, C_scales, F), "S": (S_words, S_scales, F)}
        weight_scales = {}
        weight_words = {}

        def clear_scales(name, first, last):
            width = weights[name][2]
            rows = sb.tile([P, (last - first) * PASSES * width], U8, name="%s_scales%d" % (name, first), align_bytes=64)
            nc.vector.memset(rows[:].bitcast(I32), 0)
            for mic in range(first, last):
                weight_scales[name, mic] = (rows, first)

        def load_scales(name, first, last):
            scales, width = weights[name][1:]
            rows = weight_scales[name, first][0]
            for quad in range(QUADS):
                nc.sync.dma_start(
                    out=rows[32 * quad : 32 * quad + 4, :].bitcast(I32).rearrange("r (g n) -> r g n", n=width // 4),
                    in_=scales[PASSES * first : PASSES * last, 4 * quad : 4 * quad + 4, :]
                    .bitcast(I32)
                    .rearrange("g r n -> r g n"),
                )

        def load_words(name, mic):
            words, width = weights[name][0], weights[name][2]
            packed = sb.tile([P, PASSES * 2 * width], U8, name="%s_words%d" % (name, mic), align_bytes=64)
            nc.sync.dma_start(
                out=packed[:].bitcast(I32).rearrange("p (g n) -> p g n", g=PASSES),
                in_=words[PASSES * mic : PASSES * (mic + 1)].bitcast(I32).rearrange("g p n -> p g n"),
            )
            weight_words[name, mic] = packed

        frame_bytes = {}
        frame_scales = {}
        byte_rows = X_bytes.rearrange("g (t p) k -> p (g t) k", p=P)
        scale_rows = X_scale.rearrange("g (t p) b -> p (g t) b", p=P)

        def load_frames(first, last):
            raw = sb.tile([P, last - first, L], U8, name="frame_bytes%d" % first, align_bytes=64)
            nc.sync.dma_start(out=raw[:], in_=byte_rows[:, first:last, :])
            for i in range(first, last):
                frame_bytes[i] = raw[:, i - first, :]

        def load_frame_scales(first, last):
            scales = sb.tile([P, last - first, L // Q], F32, name="frame_scales%d" % first)
            nc.sync.dma_start(out=scales[:], in_=scale_rows[:, first:last, :])
            for i in range(first, last):
                frame_scales[i] = scales[:, i - first, :]

        window_cols = sb.tile([P, G, L // P], BF16, name="window_cols")
        gain_cols = sb.tile([P, G, F // P], BF16, name="gain_cols")

        clear_scales("A", 0, 1)
        clear_scales("C", 0, G)
        clear_scales("S", 0, G)
        load_frames(0, 1)
        load_frame_scales(0, TILES_PER_MIC)
        load_frames(1, TILES_PER_MIC)
        nc.sync.dma_start(out=window_cols[:], in_=window.rearrange("g (p c) -> p g c", p=P))
        load_scales("A", 0, 1)
        load_words("A", 0)
        load_frame_scales(TILES_PER_MIC, TILES)
        load_frames(TILES_PER_MIC, 2 * TILES_PER_MIC)
        nc.sync.dma_start(out=gain_cols[:], in_=gain.rearrange("g (p c) -> p g c", p=P))
        load_frames(2 * TILES_PER_MIC, TILES)
        load_words("C", 0)
        load_words("S", 0)
        load_scales("C", 0, G)
        load_scales("S", 0, G)

        def load_later_weights():
            clear_scales("A", 1, G)
            load_scales("A", 1, G)
            for mic in range(1, G):
                for name in weights:
                    load_words(name, mic)

        window_rows = ring("window_rows", G, [P, L], BF16)
        gain_rows = ring("gain_rows", G // 2, [P, 2 * F], BF16)
        x_pairs = [ring("x_pairs%d_" % g, WIDEN_AHEAD, [P, K_PASS], BF16) for g in range(PASSES)]
        x_quads = ring("x_quads", 3, [P, L], BF16)
        x_codes = ring("x_codes", 3, [P, PASSES * P], U32)
        x_scales = ring("x_scales", 3, [P, PASSES * P], U8)
        h_pairs = [ring("h_pairs%d_" % g, 3, [P, K_PASS], BF16) for g in range(PASSES)]
        h_quads = ring("h_quads", 3, [P, L], BF16)
        h_codes = ring("h_codes", 3, [P, PASSES * P], U32)
        h_scales = ring("h_scales", 3, [P, PASSES * P], U8)
        re_sq = ring("re_sq", 3, [P, F], F32)
        im_sq = ring("im_sq", 3, [P, F], F32)
        power = ring("power", 3, [P, F], F32)
        magnitude = ring("magnitude", 3, [P, F], F32)
        y_full = ring("y_full", 4, [P, F], F32)
        y_pairs = ring("y_pairs", 3, [P, F], BF16)
        y_quads = ring("y_quads", 3, [P, F], BF16)
        y_codes = sb.tile([P, TILES * P], U32, name="y_codes", align_bytes=64)
        y_scales = sb.tile([P, TILES * P], U8, name="y_scales", align_bytes=64)

        x_bank = ps.tile([P, BANK], F32, name="x_bank")
        h_banks = [ps.tile([P, BANK], F32, name="h_bank%d" % j) for j in range(2)]
        y_bank = ps.tile([P, BANK], F32, name="y_bank")
        a_banks = [ps.tile([P, BANK], F32, name="a_bank%d" % j) for j in range(2)]
        spec_banks = [ps.tile([P, BANK], F32, name="spec_bank%d" % j) for j in range(2)]

        def in_k_order(ap):
            return ap.rearrange("p (q u e) -> p u q e", u=2, e=2)

        def in_pair_order(ap):
            return ap.rearrange("p (u q e) -> p u q e", u=2, e=2)

        def turn(bank, halves):
            for g, half in enumerate(halves):
                pairs = half[:].bitcast(F32)
                for u in range(2):
                    col = (2 * g + u) * P
                    nc.tensor.transpose(bank[:, col : col + P], pairs[:, u * P : (u + 1) * P], ident[:])

        def join(copy, quads, turned):
            copy(
                out=quads.bitcast(F32).rearrange("p (g r u) -> p g r u", r=P, u=2),
                in_=turned.rearrange("p (g u r) -> p g r u", r=P, u=2),
            )

        def quantize(codes, scales, quads):
            nc.vector.quantize_mx(out=codes.bitcast(FP8X4), scales=scales, in_=quads)

        def multiply(bank, codes, scales, name, i, col0, passes):
            mic = i // TILES_PER_MIC
            width = weights[name][2]
            rows, first = weight_scales[name, mic]
            for g in passes:
                byte0 = 2 * (g * width + col0)
                scale0 = (PASSES * (mic - first) + g) * width + col0
                nc.tensor.matmul_mx(
                    out=bank[:],
                    lhsT=codes[:, g * P : (g + 1) * P].bitcast(FP8X4),
                    lhsT_scale=scales[:, g * P : (g + 1) * P],
                    rhs=weight_words[name, mic][:, byte0 : byte0 + 2 * BANK].bitcast(FP4X4),
                    rhs_scale=rows[:, scale0 : scale0 + BANK],
                    start=(g == 0),
                    stop=(g == PASSES - 1),
                )

        def spread(bank, columns):
            for n, column in enumerate(columns):
                nc.tensor.transpose(bank[:, n * P : (n + 1) * P], column.to_broadcast([P, P]), ident[:])

        def spread_window(mic, bank):
            pairs = window_cols[:].bitcast(F32)
            spread(bank, [pairs[:, mic, c : c + 1] for c in range(4)])

        def keep_window(mic, bank):
            nc.scalar.copy(
                out=window_rows[mic][:].bitcast(F32).rearrange("p (g u l h) -> p g u l h", g=PASSES, u=2, h=2),
                in_=bank[:].rearrange("p (h u g l) -> p g u l h", g=PASSES, u=2, h=2),
            )

        def spread_gain(half, bank):
            pairs = gain_cols[:].bitcast(F32)
            spread(bank, [pairs[:, 2 * half + m, c : c + 1] for m in range(2) for c in range(2)])

        def keep_gain(half, bank):
            nc.scalar.copy(
                out=gain_rows[half][:].bitcast(F32).rearrange("p (m j c) -> p m j c", m=2, c=2),
                in_=bank[:].rearrange("p (m c j) -> p m j c", m=2, c=2),
            )

        def widen(i):
            for g in range(PASSES):
                target = slot(x_pairs[g], i)[:].rearrange("p (u q e) -> p q u e", u=2, e=2)
                for b in range(BLOCKS_PER_PASS):
                    block = BLOCKS_PER_PASS * g + b
                    codes = frame_bytes[i][:, Q * block : Q * (block + 1)].bitcast(FP8)
                    nc.vector.tensor_scalar(
                        out=target[:, (Q // 4) * b : (Q // 4) * (b + 1), :, :],
                        in0=codes.rearrange("p (q u e) -> p q u e", u=2, e=2),
                        scalar1=frame_scales[i][:, block : block + 1],
                        scalar2=None,
                        op0=ALU.mult,
                    )

        def turn_x(i, bank=x_bank):
            turn(bank, [slot(x_pairs[g], i) for g in range(PASSES)])

        def join_x(i, bank=x_bank):
            join(nc.scalar.copy, slot(x_quads, i)[:], bank[:])

        def quantize_x(i):
            quantize(slot(x_codes, i)[:], slot(x_scales, i)[:], slot(x_quads, i)[:])

        def correct(i, banks=a_banks):
            for n, bank in enumerate(banks):
                multiply(bank, slot(x_codes, i), slot(x_scales, i), "A", i, n * BANK, range(PASSES))

        def apply_window(i, g, banks=a_banks):
            nc.vector.tensor_tensor(
                out=in_pair_order(slot(h_pairs[g], i)[:]),
                in0=in_k_order(banks[g][:]),
                in1=in_pair_order(window_rows[i // TILES_PER_MIC][:, g * K_PASS : (g + 1) * K_PASS]),
                op=ALU.mult,
            )

        def turn_h(i):
            turn(slot(h_banks, i), [slot(h_pairs[g], i) for g in range(PASSES)])

        def join_h(i):
            join(nc.scalar.copy, slot(h_quads, i)[:], slot(h_banks, i)[:])

        def quantize_h(i):
            quantize(slot(h_codes, i)[:], slot(h_scales, i)[:], slot(h_quads, i)[:])

        def transform(i, banks=spec_banks, passes=range(PASSES)):
            for bank, name in zip(banks, ("C", "S")):
                multiply(bank, slot(h_codes, i), slot(h_scales, i), name, i, 0, passes)

        def square_re(i, banks=spec_banks):
            nc.scalar.activation(out=slot(re_sq, i)[:], in_=banks[0][:], func=ACT.Square)

        def square_im(i, banks=spec_banks):
            nc.scalar.activation(out=slot(im_sq, i)[:], in_=banks[1][:], func=ACT.Square)

        def add_squares(i):
            nc.vector.tensor_tensor(out=slot(power, i)[:], in0=slot(re_sq, i)[:], in1=slot(im_sq, i)[:], op=ALU.add)

        def root(i):
            nc.scalar.activation(out=slot(magnitude, i)[:], in_=slot(power, i)[:], func=ACT.Sqrt)

        def apply_gain(i):
            mic, t = divmod(i, TILES_PER_MIC)
            col0 = (mic % 2) * F
            nc.vector.tensor_tensor(
                out=slot(y_full, i)[:], in0=slot(magnitude, i)[:], in1=gain_rows[mic // 2][:, col0 : col0 + F], op=ALU.mult
            )
            nc.sync.dma_start(out=out_0[mic, P * t : P * (t + 1), :], in_=slot(y_full, i)[:])

        def round_y(i, copy):
            copy(out=in_pair_order(slot(y_pairs, i)[:]), in_=in_k_order(slot(y_full, i)[:]))

        def turn_y(i, bank=y_bank):
            turn(bank, [slot(y_pairs, i)])

        def join_y(i, copy, bank=y_bank):
            join(copy, slot(y_quads, i)[:], bank[:, 0 : 2 * P])

        code_rows = out_1[0].rearrange("p m t -> p (m t)").bitcast(I32)

        def store_codes(first, last):
            nc.sync.dma_start(out=code_rows[:, P * first : P * last], in_=y_codes[:, P * first : P * last].bitcast(I32))

        def quantize_y(i):
            quantize(y_codes[:, P * i : P * (i + 1)], y_scales[:, P * i : P * (i + 1)], slot(y_quads, i)[:])
            if i < TILES - TILES_PER_MIC and (i + 1) % TILES_PER_MIC == 0:
                store_codes(i + 1 - TILES_PER_MIC, i + 1)

        on_scalar, on_vector = nc.scalar.copy, nc.vector.tensor_copy

        widen(0)
        spread_window(0, spec_banks[0])
        keep_window(0, spec_banks[0])
        turn_x(0)
        widen(1)
        join_x(0)
        turn_x(1, h_banks[0])
        widen(2)
        load_later_weights()
        join_x(1, h_banks[0])
        turn_x(2, h_banks[1])
        quantize_x(0)
        spread_window(1, spec_banks[1])
        join_x(2, h_banks[1])
        keep_window(1, spec_banks[1])
        widen(3)
        quantize_x(1)
        quantize_x(2)
        correct(0)
        correct(1, spec_banks)
        widen(4)
        widen(5)
        apply_window(0, 0)
        apply_window(0, 1)
        turn_x(3)
        spread_gain(0, y_bank)
        turn_h(0)
        join_x(3)
        apply_window(1, 0, spec_banks)
        apply_window(1, 1, spec_banks)
        widen(6)
        join_h(0)
        keep_gain(0, y_bank)
        correct(2)
        quantize_h(0)
        quantize_x(3)
        turn_h(1)
        spread_window(2, h_banks[0])
        apply_window(2, 0)
        apply_window(2, 1)
        widen(7)
        transform(0)
        join_h(1)
        keep_window(2, h_banks[0])
        square_re(0)

        late_spreads = {
            FIRST_STEP: (spread_window, keep_window, G - 1),
            FIRST_STEP + 1: (spread_gain, keep_gain, 1),
        }
        last = TILES - 1
        for s in range(FIRST_STEP, TILES):
            widening = s + WIDEN_AHEAD <= last
            if s < last:
                turn_x(s + 1)
            if s >= 5:
                turn_y(s - 5)
            if s in late_spreads:
                late_spreads[s][0](late_spreads[s][2], y_bank)
            turn_h(s - 1)
            square_im(s - 3)
            quantize_h(s - 2)
            if s < last:
                join_x(s + 1)
            if widening:
                widen(s + WIDEN_AHEAD)
            correct(s)
            add_squares(s - 3)
            if s >= 5:
                join_y(s - 5, on_scalar)
            if s in late_spreads:
                late_spreads[s][1](late_spreads[s][2], y_bank)
            join_h(s - 1)
            if s < last:
                quantize_x(s + 1)
            apply_window(s, 0)
            transform(s - 2)
            root(s - 3)
            apply_window(s, 1)
            if s < last:
                if s >= 4:
                    round_y(s - 4, on_scalar if widening else on_vector)
                if s >= 5:
                    quantize_y(s - 5)
                apply_gain(s - 3)
                square_re(s - 2)

        pass_banks = [slot(h_banks, last), x_bank]

        def join_last(g):
            join(on_scalar, slot(h_quads, last)[:, g * K_PASS : (g + 1) * K_PASS], pass_banks[g][:, 0 : 2 * P])

        def quantize_last(g):
            quantize(
                slot(h_codes, last)[:, g * P : (g + 1) * P],
                slot(h_scales, last)[:, g * P : (g + 1) * P],
                slot(h_quads, last)[:, g * K_PASS : (g + 1) * K_PASS],
            )

        quantize_h(last - 1)
        for g in range(PASSES):
            turn(pass_banks[g], [slot(h_pairs[g], last)])
        square_re(last - 2)
        round_y(last - 4, on_vector)
        square_im(last - 2)
        transform(last - 1)
        join_last(0)
        join_last(1)
        apply_gain(last - 3)
        quantize_y(last - 5)
        add_squares(last - 2)
        quantize_last(0)
        quantize_last(1)
        turn_y(last - 4)
        for g in range(PASSES):
            transform(last, a_banks, [g])
        square_re(last - 1)
        round_y(last - 3, on_vector)
        square_im(last - 1)
        join_y(last - 4, on_vector)
        root(last - 2)
        turn_y(last - 3)
        add_squares(last - 1)
        quantize_y(last - 4)
        square_re(last, a_banks)
        apply_gain(last - 2)
        square_im(last, a_banks)
        join_y(last - 3, on_vector)
        root(last - 1)
        round_y(last - 2, on_vector)
        add_squares(last)
        turn_y(last - 2)
        quantize_y(last - 3)
        apply_gain(last - 1)
        root(last)
        join_y(last - 2, on_scalar)
        round_y(last - 1, on_vector)
        apply_gain(last)
        turn_y(last - 1, x_bank)
        quantize_y(last - 2)
        round_y(last, on_vector)
        join_y(last - 1, on_scalar, x_bank)
        turn_y(last)
        quantize_y(last - 1)
        store_codes(TILES - TILES_PER_MIC, last)
        join_y(last, on_vector)
        quantize_y(last)
        store_codes(last, TILES)

        for quad in range(QUADS):
            queue = nc.scalar if quad % 2 == 0 else nc.sync
            queue.dma_start(
                out=out_2[0, 4 * quad : 4 * quad + 4, :].bitcast(I32),
                in_=y_scales[32 * quad : 32 * quad + 4, :].bitcast(I32),
            )
